import numpy as np
import ml_dtypes


def mxq(x, axis, fmt="e4m3"):
    dtype, down = {"e4m3": (ml_dtypes.float8_e4m3fn, 7), "e5m2": (ml_dtypes.float8_e5m2, 14)}[fmt]
    v = np.moveaxis(np.asarray(x, np.float32).astype(ml_dtypes.bfloat16).astype(np.float64), axis, -1)
    blocks = v.reshape(v.shape[:-1] + (-1, 32))
    amax = np.abs(blocks).max(-1, keepdims=True)
    byte = np.maximum(np.where(amax > 0, np.frexp(amax)[1] - 1 + 127, 0) - down, 1)
    scale = np.exp2(byte - 127.0)
    codes = (blocks / scale).astype(np.float32).astype(dtype).astype(np.float64)
    return np.moveaxis((codes * scale).reshape(v.shape), -1, axis)


WIDE = False


def mx_kscale(k):
    if not WIDE:
        return np.ones(k)
    levels = np.array([10, -10, 5, -5, 0])
    if k % 512:
        return np.exp2(np.random.permutation(np.resize(levels, k // 32))).repeat(32)
    a = np.empty((k // 512, 16))
    for p in range(k // 512):
        a[p, :8] = np.random.permutation(np.resize(levels, 8))
        for g in range(8):
            far = levels[np.abs(levels - a[p, g]) >= 10]
            a[p, g + 8] = far[np.random.randint(len(far))]
    return np.exp2(a.ravel()).repeat(32)


def f64(x):
    return np.asarray(x).astype(np.float64)


def striped(idx):
    return np.tile(idx.reshape(-1, 16).T, (8, 1)).astype(np.uint16)


def unstriped(offs):
    return offs[:16].T.reshape(-1).astype(np.int64)


def pack_weight(w):
    k, n = w.shape
    w = f64(np.asarray(w, np.float32).astype(ml_dtypes.bfloat16)).reshape(k // 32, 32, n)
    amax = np.abs(w).max(1)
    byte = np.clip(np.where(amax > 0, np.frexp(amax)[1] - 1 + 127 - 7, 1), 1, 254)
    scaled = (w * np.exp2(127.0 - byte)[:, None, :]).reshape(k, n).astype(np.float32)
    words = np.ascontiguousarray(scaled.reshape(k // 512, 128, 4, n).transpose(0, 1, 3, 2)).astype(ml_dtypes.float8_e4m3fn).view(np.uint8)
    return words, np.ascontiguousarray(byte.astype(np.uint8).reshape(k // 512, 16, n))


def unpack_weight(words, scales):
    g, p, n, _ = words.shape
    vals = np.ascontiguousarray(words).view(ml_dtypes.float8_e4m3fn).astype(np.float64) * np.repeat(np.exp2(scales.astype(np.float64) - 127.0), 8, axis=1)[..., None]
    return vals.transpose(0, 1, 3, 2).reshape(g * 512, n)


def relu(v):
    return np.maximum(v, 0.0)


def sigmoid(v):
    return 1.0 / (1.0 + np.exp(-np.maximum(v, -700.0)))


K, T, S, H, N, U = 512, 1024, 512, 512, 128, 1024
P = 2 ** 7


def setup_inputs():
    n = np.random.standard_normal
    s = mx_kscale(K)[:, None]
    u = mx_kscale(H)
    packed_xT = pack_weight(n((K, T)) * s)
    return {
        "x_words": packed_xT[0],
        "x_scales": packed_xT[1],
        "mem": (n((H, U)) * u[:, None]).astype(np.float32),
        "gap": (np.tile(np.random.uniform(0.1, 2.0, S), (P, 1))).astype(np.float32),
        "rate": (0.7 * n((H, 1))).astype(np.float32),
        "off": (0.3 * n((H, 1))).astype(np.float32),
        "w1": (n((K, N)) / np.sqrt(2 * K) / s).astype(np.float32),
        "rr": (n((H, N)) / np.sqrt(2 * H) / u[:, None]).astype(np.float32),
        "offs": striped(np.random.permutation(T)[:S]),
        "slot": striped(np.random.permutation(U)[:S]),
    }


def reference(x_words, x_scales, mem, gap, rate, off, w1, rr, offs, slot):
    fade = np.exp(-1.0 * (relu(f64(rate) * f64(gap)[:1] + f64(off))))
    h = f64(mem)[:, unstriped(slot)] * fade
    xq = unpack_weight(x_words, x_scales)[:, unstriped(offs)]
    return sigmoid(mxq(f64(rr), 0, "e4m3").T @ mxq(h, 0, "e4m3") + mxq(f64(w1), 0, "e4m3").T @ xq)

@@ -1,0 +1,149 @@
+from contextlib import ExitStack
+
+import concourse.mybir as mybir
+
+K, T, S, H, N, U = 512, 1024, 512, 512, 128, 1024
+FLOPS = 2 * (K + H) * N * S
+
+F32 = mybir.dt.float32
+BF16 = mybir.dt.bfloat16
+I32 = mybir.dt.int32
+U32 = mybir.dt.uint32
+U16 = mybir.dt.uint16
+U8 = mybir.dt.uint8
+FP8X4 = mybir.dt.float8_e4m3fn_x4
+ALU = mybir.AluOpType
+ACT = mybir.ActivationFunctionType
+
+P = 128
+PACK = 4
+HALF = S // 2
+
+
+def interleave(copy, dst, src):
+    copy(
+        out=dst.rearrange("p (c i) t -> p c t i", i=4),
+        in_=src.rearrange("p t (c i) -> p c t i", i=4),
+    )
+
+
+def tile_picked_ygrud_gate_p_kernel(tc, x_words, x_scales, mem, gap, rate, off, w1, rr, offs, slot, out):
+    nc = tc.nc
+    with ExitStack() as ctx:
+        keep = ctx.enter_context(tc.tile_pool(name="keep", bufs=1))
+        psum = ctx.enter_context(tc.psum_pool(name="psum", bufs=1))
+
+        slot_sb = keep.tile([P, S // 16], U16, name="slot_sb")
+        offs_sb = keep.tile([P, S // 16], U16, name="offs_sb")
+        gap_sb = keep.tile([P, S], F32, name="gap_sb")
+        rate_sb = keep.tile([P, PACK], F32, name="rate_sb")
+        off_sb = keep.tile([P, PACK], F32, name="off_sb")
+        mem_sb = [keep.tile([P, U], F32, name=f"mem_sb{t}") for t in range(PACK)]
+        rr_sb = keep.tile([P, PACK, N], F32, name="rr_sb")
+        w1_sb = keep.tile([P, PACK, N], F32, name="w1_sb")
+        words_sb = keep.tile([P, T], I32, name="words_sb")
+        scales_sb = keep.tile([P, T], U8, name="scales_sb")
+
+        mem_rows = mem.rearrange("(p t) u -> p t u", t=PACK)
+        nc.scalar.dma_start(out=off_sb[:], in_=off.rearrange("(p t) o -> p (t o)", t=PACK))
+        nc.scalar.dma_start(out=rate_sb[:], in_=rate.rearrange("(p t) o -> p (t o)", t=PACK))
+        nc.sync.dma_start(out=gap_sb[:], in_=gap)
+        nc.sync.dma_start(slot_sb[:], slot)
+        nc.sync.dma_start(out=mem_sb[0][:], in_=mem_rows[:, 0, :])
+        nc.vector.memset(scales_sb[:].bitcast(I32), 0)
+        for t in range(1, PACK - 1):
+            nc.sync.dma_start(out=mem_sb[t][:], in_=mem_rows[:, t, :])
+        nc.sync.dma_start(offs_sb[:], offs)
+        for q in range(4):
+            nc.sync.dma_start(
+                out=scales_sb[32 * q : 32 * q + 4, :].bitcast(I32),
+                in_=x_scales[0, 4 * q : 4 * q + 4, :].bitcast(I32),
+            )
+        nc.sync.dma_start(out=rr_sb[:], in_=rr.rearrange("(p t) n -> p t n", t=PACK))
+        nc.sync.dma_start(out=w1_sb[:], in_=w1.rearrange("(p t) n -> p t n", t=PACK))
+        nc.sync.dma_start(out=mem_sb[PACK - 1][:], in_=mem_rows[:, PACK - 1, :])
+        nc.sync.dma_start(out=words_sb[:], in_=x_words[0].rearrange("p c r -> p (c r)").bitcast(I32))
+
+        warm0 = keep.tile([P, 1], F32, name="warm0")
+        nc.gpsimd.memset(warm0[:], 0.0)
+        nc.scalar.activation(warm0[:], warm0[:], ACT.Exp)
+        neg_off = keep.tile([P, PACK], F32, name="neg_off")
+        nc.vector.tensor_scalar(neg_off[:], off_sb[:], -1.0, None, ALU.mult)
+        fade = []
+        for t in range(PACK):
+            clamped = keep.tile([P, S], F32, name=f"clamped{t}")
+            fade_t = keep.tile([P, S], F32, name=f"fade{t}")
+            if t == 0:
+                nc.scalar.activation(
+                    clamped[:], gap_sb[:], ACT.Relu, bias=off_sb[:, t : t + 1], scale=rate_sb[:, t : t + 1]
+                )
+                nc.scalar.activation(fade_t[:], clamped[:], ACT.Exp, scale=-1.0)
+            else:
+                nc.vector.tensor_scalar(
+                    clamped[:], gap_sb[:], rate_sb[:, t : t + 1], neg_off[:, t : t + 1], ALU.mult, ALU.max
+                )
+                nc.scalar.activation(fade_t[:], clamped[:], ACT.Exp, bias=neg_off[:, t : t + 1], scale=-1.0)
+            fade.append(fade_t)
+        warm = keep.tile([P, 1], F32, name="warm")
+        nc.scalar.activation(warm[:], fade[PACK - 1][:, 0:1], ACT.Sigmoid)
+
+        h_rows = keep.tile([P, PACK, S], F32, name="h_all")
+        for t in range(PACK - 1):
+            nc.vector.tensor_tensor(h_rows[:, t, :], mem_sb[t][:].indirect(slot_sb[:]), fade[t][:], ALU.mult)
+        x_codes = keep.tile([P, S], U32, name="x_codes", align_bytes=64)
+        x_exps = keep.tile([P, S], U8, name="x_exps", align_bytes=64)
+        nc.vector.tensor_copy(x_exps[:], scales_sb[:].indirect(offs_sb[:]))
+        t = PACK - 1
+        for a in range(2):
+            nc.vector.tensor_tensor(
+                h_rows[:, t, a * HALF : (a + 1) * HALF],
+                mem_sb[t][:].indirect(slot_sb[:, a * HALF // 16 : (a + 1) * HALF // 16]),
+                fade[t][:, a * HALF : (a + 1) * HALF],
+                ALU.mult,
+            )
+        nc.vector.tensor_copy(x_codes[:], words_sb[:].bitcast(U32).indirect(offs_sb[:]))
+
+        w_bf = keep.tile([P, 2 * N, PACK], BF16, name="w_bf", align_bytes=64)
+        h_bf = [keep.tile([P, HALF, PACK], BF16, name=f"h_bf{a}", align_bytes=64) for a in range(2)]
+        interleave(nc.scalar.copy, w_bf[:, 0:N, :], rr_sb[:])
+        interleave(nc.scalar.copy, w_bf[:, N : 2 * N, :], w1_sb[:])
+        for a in range(2):
+            interleave(nc.scalar.copy, h_bf[a][:], h_rows[:, :, a * HALF : (a + 1) * HALF])
+
+        w_codes = keep.tile([P, 2 * N], U32, name="w_codes", align_bytes=64)
+        w_exps = keep.tile([P, 2 * N], U8, name="w_exps", align_bytes=64)
+        nc.vector.quantize_mx(
+            out=w_codes[:].bitcast(FP8X4), scales=w_exps[:], in_=w_bf[:].rearrange("p n t -> p (n t)")
+        )
+
+        acc = [psum.tile([N, HALF], F32, name=f"acc{a}") for a in range(2)]
+        for a in range(2):
+            cols = slice(a * HALF, (a + 1) * HALF)
+            nc.tensor.matmul_mx(
+                out=acc[a][:],
+                lhsT=w_codes[:, N : 2 * N].bitcast(FP8X4),
+                lhsT_scale=w_exps[:, N : 2 * N],
+                rhs=x_codes[:, cols].bitcast(FP8X4),
+                rhs_scale=x_exps[:, cols],
+                start=True,
+                stop=False,
+            )
+        for a in range(2):
+            cols = slice(a * HALF, (a + 1) * HALF)
+            h_codes = keep.tile([P, HALF], U32, name=f"h_codes{a}", align_bytes=64)
+            h_exps = keep.tile([P, HALF], U8, name=f"h_exps{a}", align_bytes=64)
+            nc.vector.quantize_mx(
+                out=h_codes[:].bitcast(FP8X4), scales=h_exps[:], in_=h_bf[a][:].rearrange("p j t -> p (j t)")
+            )
+            nc.tensor.matmul_mx(
+                out=acc[a][:],
+                lhsT=w_codes[:, 0:N].bitcast(FP8X4),
+                lhsT_scale=w_exps[:, 0:N],
+                rhs=h_codes[:].bitcast(FP8X4),
+                rhs_scale=h_exps[:],
+                start=False,
+                stop=True,
+            )
+            gate = keep.tile([N, HALF], F32, name=f"gate{a}")
+            nc.scalar.activation(gate[:], acc[a][:], ACT.Sigmoid)
+            nc.sync.dma_start(out=out[:, cols], in_=gate[:])

@@ -1,6 +1,7 @@
 from contextlib import ExitStack
 
 import concourse.mybir as mybir
+from concourse.masks import make_identity
 
 K, T, S, H, N, U = 512, 1024, 512, 512, 128, 1024
 FLOPS = 2 * (K + H) * N * S
@@ -18,6 +19,7 @@ ACT = mybir.ActivationFunctionType
 P = 128
 PACK = 4
 HALF = S // 2
+PIECES = [(0, 256), (256, 384), (384, 512)]
 
 
 def interleave(copy, dst, src):
@@ -31,11 +33,12 @@ def tile_picked_ygrud_gate_p_kernel(tc, x_words, x_scales, mem, gap, rate, off, 
     nc = tc.nc
     with ExitStack() as ctx:
         keep = ctx.enter_context(tc.tile_pool(name="keep", bufs=1))
+        ring = ctx.enter_context(tc.tile_pool(name="ring", bufs=2))
         psum = ctx.enter_context(tc.psum_pool(name="psum", bufs=1))
 
         slot_sb = keep.tile([P, S // 16], U16, name="slot_sb")
         offs_sb = keep.tile([P, S // 16], U16, name="offs_sb")
-        gap_sb = keep.tile([P, S], F32, name="gap_sb")
+        gap_col = keep.tile([P, PACK], F32, name="gap_col")
         rate_sb = keep.tile([P, PACK], F32, name="rate_sb")
         off_sb = keep.tile([P, PACK], F32, name="off_sb")
         mem_sb = [keep.tile([P, U], F32, name=f"mem_sb{t}") for t in range(PACK)]
@@ -43,107 +46,108 @@ def tile_picked_ygrud_gate_p_kernel(tc, x_words, x_scales, mem, gap, rate, off, 
         w1_sb = keep.tile([P, PACK, N], F32, name="w1_sb")
         words_sb = keep.tile([P, T], I32, name="words_sb")
         scales_sb = keep.tile([P, T], U8, name="scales_sb")
+        x_exps = keep.tile([P, S], U8, name="x_exps", align_bytes=64)
 
-        mem_rows = mem.rearrange("(p t) u -> p t u", t=PACK)
-        nc.scalar.dma_start(out=off_sb[:], in_=off.rearrange("(p t) o -> p (t o)", t=PACK))
-        nc.scalar.dma_start(out=rate_sb[:], in_=rate.rearrange("(p t) o -> p (t o)", t=PACK))
-        nc.sync.dma_start(out=gap_sb[:], in_=gap)
-        nc.sync.dma_start(slot_sb[:], slot)
-        nc.sync.dma_start(out=mem_sb[0][:], in_=mem_rows[:, 0, :])
         nc.vector.memset(scales_sb[:].bitcast(I32), 0)
-        for t in range(1, PACK - 1):
-            nc.sync.dma_start(out=mem_sb[t][:], in_=mem_rows[:, t, :])
+        nc.vector.memset(x_exps[:].bitcast(I32), 0)
+        mem_rows = mem.rearrange("(p t) u -> p t u", t=PACK)
+        nc.scalar.dma_start(out=gap_col[:], in_=gap[0:1, :].rearrange("o (p c) -> p (o c)", c=PACK))
+        nc.scalar.dma_start(out=rate_sb[:], in_=rate.rearrange("(p t) o -> p (t o)", t=PACK))
+        nc.scalar.dma_start(out=off_sb[:], in_=off.rearrange("(p t) o -> p (t o)", t=PACK))
         nc.sync.dma_start(offs_sb[:], offs)
+        nc.sync.dma_start(out=scales_sb[0:16, :].bitcast(I32), in_=x_scales[0].bitcast(I32))
+        nc.sync.dma_start(out=words_sb[:], in_=x_words[0].rearrange("p c r -> p (c r)").bitcast(I32))
+        nc.sync.dma_start(slot_sb[:], slot)
+        for t in range(PACK):
+            nc.sync.dma_start(out=mem_sb[t][:], in_=mem_rows[:, t, :])
+        nc.sync.dma_start(out=w1_sb[:], in_=w1.rearrange("(p t) n -> p t n", t=PACK))
+        nc.sync.dma_start(out=rr_sb[:], in_=rr.rearrange("(p t) n -> p t n", t=PACK))
+
+        warm = keep.tile([P, 1], F32, name="warm")
+        nc.gpsimd.memset(warm[:], 0.0)
+        nc.scalar.activation(warm[:], warm[:], ACT.Exp)
+
+        ident = keep.tile([P, P], F32, name="ident")
+        make_identity(nc, ident[:])
+        gap_ps = psum.tile([P, PACK, P], F32, name="gap_ps")
+        for c in range(PACK):
+            nc.tensor.transpose(gap_ps[:, c, :], gap_col[:, c : c + 1].to_broadcast([P, P]), ident[:])
+
+        picked_exps = keep.tile([P, S], U8, name="picked_exps")
+        nc.vector.tensor_copy(picked_exps[:], scales_sb[:].indirect(offs_sb[:]))
         for q in range(4):
             nc.sync.dma_start(
-                out=scales_sb[32 * q : 32 * q + 4, :].bitcast(I32),
-                in_=x_scales[0, 4 * q : 4 * q + 4, :].bitcast(I32),
+                out=x_exps[32 * q : 32 * q + 4, :].bitcast(I32), in_=picked_exps[4 * q : 4 * q + 4, :].bitcast(I32)
             )
-        nc.sync.dma_start(out=rr_sb[:], in_=rr.rearrange("(p t) n -> p t n", t=PACK))
-        nc.sync.dma_start(out=w1_sb[:], in_=w1.rearrange("(p t) n -> p t n", t=PACK))
-        nc.sync.dma_start(out=mem_sb[PACK - 1][:], in_=mem_rows[:, PACK - 1, :])
-        nc.sync.dma_start(out=words_sb[:], in_=x_words[0].rearrange("p c r -> p (c r)").bitcast(I32))
-
-        warm0 = keep.tile([P, 1], F32, name="warm0")
-        nc.gpsimd.memset(warm0[:], 0.0)
-        nc.scalar.activation(warm0[:], warm0[:], ACT.Exp)
-        neg_off = keep.tile([P, PACK], F32, name="neg_off")
-        nc.vector.tensor_scalar(neg_off[:], off_sb[:], -1.0, None, ALU.mult)
-        fade = []
-        for t in range(PACK):
-            clamped = keep.tile([P, S], F32, name=f"clamped{t}")
-            fade_t = keep.tile([P, S], F32, name=f"fade{t}")
-            if t == 0:
-                nc.scalar.activation(
-                    clamped[:], gap_sb[:], ACT.Relu, bias=off_sb[:, t : t + 1], scale=rate_sb[:, t : t + 1]
-                )
-                nc.scalar.activation(fade_t[:], clamped[:], ACT.Exp, scale=-1.0)
-            else:
-                nc.vector.tensor_scalar(
-                    clamped[:], gap_sb[:], rate_sb[:, t : t + 1], neg_off[:, t : t + 1], ALU.mult, ALU.max
-                )
-                nc.scalar.activation(fade_t[:], clamped[:], ACT.Exp, bias=neg_off[:, t : t + 1], scale=-1.0)
-            fade.append(fade_t)
-        warm = keep.tile([P, 1], F32, name="warm")
-        nc.scalar.activation(warm[:], fade[PACK - 1][:, 0:1], ACT.Sigmoid)
-
-        h_rows = keep.tile([P, PACK, S], F32, name="h_all")
-        for t in range(PACK - 1):
-            nc.vector.tensor_tensor(h_rows[:, t, :], mem_sb[t][:].indirect(slot_sb[:]), fade[t][:], ALU.mult)
         x_codes = keep.tile([P, S], U32, name="x_codes", align_bytes=64)
-        x_exps = keep.tile([P, S], U8, name="x_exps", align_bytes=64)
-        nc.vector.tensor_copy(x_exps[:], scales_sb[:].indirect(offs_sb[:]))
-        t = PACK - 1
-        for a in range(2):
-            nc.vector.tensor_tensor(
-                h_rows[:, t, a * HALF : (a + 1) * HALF],
-                mem_sb[t][:].indirect(slot_sb[:, a * HALF // 16 : (a + 1) * HALF // 16]),
-                fade[t][:, a * HALF : (a + 1) * HALF],
-                ALU.mult,
-            )
         nc.vector.tensor_copy(x_codes[:], words_sb[:].bitcast(U32).indirect(offs_sb[:]))
 
-        w_bf = keep.tile([P, 2 * N, PACK], BF16, name="w_bf", align_bytes=64)
-        h_bf = [keep.tile([P, HALF, PACK], BF16, name=f"h_bf{a}", align_bytes=64) for a in range(2)]
-        interleave(nc.scalar.copy, w_bf[:, 0:N, :], rr_sb[:])
-        interleave(nc.scalar.copy, w_bf[:, N : 2 * N, :], w1_sb[:])
-        for a in range(2):
-            interleave(nc.scalar.copy, h_bf[a][:], h_rows[:, :, a * HALF : (a + 1) * HALF])
+        h_rows = keep.tile([P, PACK, S], F32, name="h_rows")
+        for t in range(PACK):
+            clamped = []
+            for a in range(2):
+                clamped.append(ring.tile([P, HALF], F32, name="clamped"))
+                nc.scalar.activation(
+                    clamped[a][:].rearrange("q (p c) -> q p c", c=PACK),
+                    gap_ps[:, :, a * P // 2 : (a + 1) * P // 2].rearrange("q c p -> q p c"),
+                    ACT.Relu,
+                    bias=off_sb[:, t : t + 1],
+                    scale=rate_sb[:, t : t + 1],
+                )
+            fade = keep.tile([P, S], F32, name=f"fade{t}", align_bytes=64)
+            for a in range(2):
+                nc.scalar.activation(fade[:, a * HALF : (a + 1) * HALF], clamped[a][:], ACT.Exp, scale=-1.0)
+            for lo, hi in [(0, HALF), (HALF, S)] if t == PACK - 1 else [(0, S)]:
+                nc.vector.tensor_tensor(
+                    h_rows[:, t, lo:hi],
+                    mem_sb[t][:].indirect(slot_sb[:, lo // 16 : hi // 16]),
+                    fade[:, lo:hi],
+                    ALU.mult,
+                )
 
+        w_bf = keep.tile([P, 2 * N, PACK], BF16, name="w_bf", tag="fade3", align_bytes=64)
+        interleave(nc.vector.tensor_copy, w_bf[:, 0:N, :], w1_sb[:])
+        interleave(nc.vector.tensor_copy, w_bf[:, N : 2 * N, :], rr_sb[:])
         w_codes = keep.tile([P, 2 * N], U32, name="w_codes", align_bytes=64)
         w_exps = keep.tile([P, 2 * N], U8, name="w_exps", align_bytes=64)
         nc.vector.quantize_mx(
             out=w_codes[:].bitcast(FP8X4), scales=w_exps[:], in_=w_bf[:].rearrange("p n t -> p (n t)")
         )
 
-        acc = [psum.tile([N, HALF], F32, name=f"acc{a}") for a in range(2)]
-        for a in range(2):
-            cols = slice(a * HALF, (a + 1) * HALF)
+        h_bf = []
+        for lo, hi in PIECES:
+            h_bf.append(keep.tile([P, hi - lo, PACK], BF16, name=f"h_bf{lo}", align_bytes=64))
+            interleave(nc.scalar.copy, h_bf[-1][:], h_rows[:, :, lo:hi])
+
+        acc = []
+        for lo, hi in PIECES:
+            acc.append(psum.tile([N, hi - lo], F32, name=f"acc{lo}"))
             nc.tensor.matmul_mx(
-                out=acc[a][:],
-                lhsT=w_codes[:, N : 2 * N].bitcast(FP8X4),
-                lhsT_scale=w_exps[:, N : 2 * N],
-                rhs=x_codes[:, cols].bitcast(FP8X4),
-                rhs_scale=x_exps[:, cols],
+                out=acc[-1][:],
+                lhsT=w_codes[:, 0:N].bitcast(FP8X4),
+                lhsT_scale=w_exps[:, 0:N],
+                rhs=x_codes[:, lo:hi].bitcast(FP8X4),
+                rhs_scale=x_exps[:, lo:hi],
                 start=True,
                 stop=False,
             )
-        for a in range(2):
-            cols = slice(a * HALF, (a + 1) * HALF)
-            h_codes = keep.tile([P, HALF], U32, name=f"h_codes{a}", align_bytes=64)
-            h_exps = keep.tile([P, HALF], U8, name=f"h_exps{a}", align_bytes=64)
+        for i, (lo, hi) in enumerate(PIECES):
+            h_codes = keep.tile([P, hi - lo], U32, name=f"h_codes{lo}", align_bytes=64)
+            h_exps = keep.tile([P, hi - lo], U8, name=f"h_exps{lo}", align_bytes=64)
             nc.vector.quantize_mx(
-                out=h_codes[:].bitcast(FP8X4), scales=h_exps[:], in_=h_bf[a][:].rearrange("p j t -> p (j t)")
+                out=h_codes[:].bitcast(FP8X4), scales=h_exps[:], in_=h_bf[i][:].rearrange("p j t -> p (j t)")
             )
             nc.tensor.matmul_mx(
-                out=acc[a][:],
-                lhsT=w_codes[:, 0:N].bitcast(FP8X4),
-                lhsT_scale=w_exps[:, 0:N],
+                out=acc[i][:],
+                lhsT=w_codes[:, N : 2 * N].bitcast(FP8X4),
+                lhsT_scale=w_exps[:, N : 2 * N],
                 rhs=h_codes[:].bitcast(FP8X4),
                 rhs_scale=h_exps[:],
                 start=False,
                 stop=True,
             )
-            gate = keep.tile([N, HALF], F32, name=f"gate{a}")
-            nc.scalar.activation(gate[:], acc[a][:], ACT.Sigmoid)
-            nc.sync.dma_start(out=out[:, cols], in_=gate[:])
+            half_tanh = keep.tile([N, hi - lo], F32, name=f"half_tanh{lo}")
+            nc.scalar.activation(half_tanh[:], acc[i][:], ACT.Tanh, scale=0.5)
+            gate = keep.tile([N, hi - lo], F32, name=f"gate{lo}")
+            nc.vector.tensor_scalar(gate[:], half_tanh[:], 0.5, 0.5, ALU.mult, ALU.add)
+            nc.sync.dma_start(out=out[:, lo:hi], in_=gate[:])

@@ -38,7 +38,8 @@ def tile_picked_ygrud_gate_p_kernel(tc, x_words, x_scales, mem, gap, rate, off, 
 
         slot_sb = keep.tile([P, S // 16], U16, name="slot_sb")
         offs_sb = keep.tile([P, S // 16], U16, name="offs_sb")
-        gap_col = keep.tile([P, PACK], F32, name="gap_col")
+        gap_col = keep.tile([P, 2], F32, name="gap_col")
+        gap_lo = keep.tile([P, HALF], F32, name="gap_lo")
         rate_sb = keep.tile([P, PACK], F32, name="rate_sb")
         off_sb = keep.tile([P, PACK], F32, name="off_sb")
         mem_sb = [keep.tile([P, U], F32, name=f"mem_sb{t}") for t in range(PACK)]
@@ -51,17 +52,19 @@ def tile_picked_ygrud_gate_p_kernel(tc, x_words, x_scales, mem, gap, rate, off, 
         nc.vector.memset(scales_sb[:].bitcast(I32), 0)
         nc.vector.memset(x_exps[:].bitcast(I32), 0)
         mem_rows = mem.rearrange("(p t) u -> p t u", t=PACK)
-        nc.scalar.dma_start(out=gap_col[:], in_=gap[0:1, :].rearrange("o (p c) -> p (o c)", c=PACK))
         nc.scalar.dma_start(out=rate_sb[:], in_=rate.rearrange("(p t) o -> p (t o)", t=PACK))
         nc.scalar.dma_start(out=off_sb[:], in_=off.rearrange("(p t) o -> p (t o)", t=PACK))
+        nc.scalar.dma_start(out=gap_col[:], in_=gap[0:1, HALF:S].rearrange("o (p c) -> p (o c)", c=2))
+        nc.sync.dma_start(out=gap_lo[:], in_=gap[:, 0:HALF])
         nc.sync.dma_start(offs_sb[:], offs)
         nc.sync.dma_start(out=scales_sb[0:16, :].bitcast(I32), in_=x_scales[0].bitcast(I32))
-        nc.sync.dma_start(out=words_sb[:], in_=x_words[0].rearrange("p c r -> p (c r)").bitcast(I32))
+        nc.sync.dma_start(out=mem_sb[0][:], in_=mem_rows[:, 0, :])
         nc.sync.dma_start(slot_sb[:], slot)
-        for t in range(PACK):
+        for t in range(1, PACK):
             nc.sync.dma_start(out=mem_sb[t][:], in_=mem_rows[:, t, :])
         nc.sync.dma_start(out=w1_sb[:], in_=w1.rearrange("(p t) n -> p t n", t=PACK))
         nc.sync.dma_start(out=rr_sb[:], in_=rr.rearrange("(p t) n -> p t n", t=PACK))
+        nc.sync.dma_start(out=words_sb[:], in_=x_words[0].rearrange("p c r -> p (c r)").bitcast(I32))
 
         warm = keep.tile([P, 1], F32, name="warm")
         nc.gpsimd.memset(warm[:], 0.0)
@@ -69,8 +72,8 @@ def tile_picked_ygrud_gate_p_kernel(tc, x_words, x_scales, mem, gap, rate, off, 
 
         ident = keep.tile([P, P], F32, name="ident")
         make_identity(nc, ident[:])
-        gap_ps = psum.tile([P, PACK, P], F32, name="gap_ps")
-        for c in range(PACK):
+        gap_ps = psum.tile([P, 2, P], F32, name="gap_ps")
+        for c in range(2):
             nc.tensor.transpose(gap_ps[:, c, :], gap_col[:, c : c + 1].to_broadcast([P, P]), ident[:])
 
         picked_exps = keep.tile([P, S], U8, name="picked_exps")
@@ -79,17 +82,16 @@ def tile_picked_ygrud_gate_p_kernel(tc, x_words, x_scales, mem, gap, rate, off, 
             nc.sync.dma_start(
                 out=x_exps[32 * q : 32 * q + 4, :].bitcast(I32), in_=picked_exps[4 * q : 4 * q + 4, :].bitcast(I32)
             )
-        x_codes = keep.tile([P, S], U32, name="x_codes", align_bytes=64)
-        nc.vector.tensor_copy(x_codes[:], words_sb[:].bitcast(U32).indirect(offs_sb[:]))
+        gap_halves = [gap_lo[:].rearrange("q (p c) -> q p c", c=2), gap_ps[:].rearrange("q c p -> q p c")]
 
-        h_rows = keep.tile([P, PACK, S], F32, name="h_rows")
+        h_rows = keep.tile([P, PACK, S], F32, name="h_rows", align_bytes=64)
         for t in range(PACK):
             clamped = []
             for a in range(2):
                 clamped.append(ring.tile([P, HALF], F32, name="clamped"))
                 nc.scalar.activation(
-                    clamped[a][:].rearrange("q (p c) -> q p c", c=PACK),
-                    gap_ps[:, :, a * P // 2 : (a + 1) * P // 2].rearrange("q c p -> q p c"),
+                    clamped[a][:].rearrange("q (p c) -> q p c", c=2),
+                    gap_halves[a],
                     ACT.Relu,
                     bias=off_sb[:, t : t + 1],
                     scale=rate_sb[:, t : t + 1],
@@ -97,7 +99,7 @@ def tile_picked_ygrud_gate_p_kernel(tc, x_words, x_scales, mem, gap, rate, off, 
             fade = keep.tile([P, S], F32, name=f"fade{t}", align_bytes=64)
             for a in range(2):
                 nc.scalar.activation(fade[:, a * HALF : (a + 1) * HALF], clamped[a][:], ACT.Exp, scale=-1.0)
-            for lo, hi in [(0, HALF), (HALF, S)] if t == PACK - 1 else [(0, S)]:
+            for lo, hi in [(0, HALF), (HALF, S)] if t in (0, PACK - 1) else [(0, S)]:
                 nc.vector.tensor_tensor(
                     h_rows[:, t, lo:hi],
                     mem_sb[t][:].indirect(slot_sb[:, lo // 16 : hi // 16]),
@@ -119,33 +121,32 @@ def tile_picked_ygrud_gate_p_kernel(tc, x_words, x_scales, mem, gap, rate, off, 
             h_bf.append(keep.tile([P, hi - lo, PACK], BF16, name=f"h_bf{lo}", align_bytes=64))
             interleave(nc.scalar.copy, h_bf[-1][:], h_rows[:, :, lo:hi])
 
-        acc = []
-        for lo, hi in PIECES:
-            acc.append(psum.tile([N, hi - lo], F32, name=f"acc{lo}"))
+        def one_pass(acc, w_cols, codes, exps, first):
             nc.tensor.matmul_mx(
-                out=acc[-1][:],
-                lhsT=w_codes[:, 0:N].bitcast(FP8X4),
-                lhsT_scale=w_exps[:, 0:N],
-                rhs=x_codes[:, lo:hi].bitcast(FP8X4),
-                rhs_scale=x_exps[:, lo:hi],
-                start=True,
-                stop=False,
+                out=acc,
+                lhsT=w_codes[:, w_cols].bitcast(FP8X4),
+                lhsT_scale=w_exps[:, w_cols],
+                rhs=codes.bitcast(FP8X4),
+                rhs_scale=exps,
+                start=first,
+                stop=not first,
             )
+
+        acc = [psum.tile([N, hi - lo], F32, name=f"acc{lo}") for lo, hi in PIECES]
         for i, (lo, hi) in enumerate(PIECES):
             h_codes = keep.tile([P, hi - lo], U32, name=f"h_codes{lo}", align_bytes=64)
             h_exps = keep.tile([P, hi - lo], U8, name=f"h_exps{lo}", align_bytes=64)
             nc.vector.quantize_mx(
                 out=h_codes[:].bitcast(FP8X4), scales=h_exps[:], in_=h_bf[i][:].rearrange("p j t -> p (j t)")
             )
-            nc.tensor.matmul_mx(
-                out=acc[i][:],
-                lhsT=w_codes[:, N : 2 * N].bitcast(FP8X4),
-                lhsT_scale=w_exps[:, N : 2 * N],
-                rhs=h_codes[:].bitcast(FP8X4),
-                rhs_scale=h_exps[:],
-                start=False,
-                stop=True,
+            one_pass(acc[i][:], slice(N, 2 * N), h_codes[:], h_exps[:], True)
+
+        x_codes = keep.tile([P, S], U32, name="x_codes", tag="h_rows", align_bytes=64)
+        for i, (lo, hi) in enumerate(PIECES):
+            nc.vector.tensor_copy(
+                x_codes[:, lo:hi], words_sb[:].bitcast(U32).indirect(offs_sb[:, lo // 16 : hi // 16])
             )
+            one_pass(acc[i][:], slice(0, N), x_codes[:, lo:hi], x_exps[:, lo:hi], False)
             half_tanh = keep.tile([N, hi - lo], F32, name=f"half_tanh{lo}")
             nc.scalar.activation(half_tanh[:], acc[i][:], ACT.Tanh, scale=0.5)
             gate = keep.tile([N, hi - lo], F32, name=f"gate{lo}")

@@ -38,8 +38,7 @@ def tile_picked_ygrud_gate_p_kernel(tc, x_words, x_scales, mem, gap, rate, off, 
 
         slot_sb = keep.tile([P, S // 16], U16, name="slot_sb")
         offs_sb = keep.tile([P, S // 16], U16, name="offs_sb")
-        gap_col = keep.tile([P, 2], F32, name="gap_col")
-        gap_lo = keep.tile([P, HALF], F32, name="gap_lo")
+        gap_col = keep.tile([P, 2, 2], F32, name="gap_col")
         rate_sb = keep.tile([P, PACK], F32, name="rate_sb")
         off_sb = keep.tile([P, PACK], F32, name="off_sb")
         mem_sb = [keep.tile([P, U], F32, name=f"mem_sb{t}") for t in range(PACK)]
@@ -54,8 +53,7 @@ def tile_picked_ygrud_gate_p_kernel(tc, x_words, x_scales, mem, gap, rate, off, 
         mem_rows = mem.rearrange("(p t) u -> p t u", t=PACK)
         nc.scalar.dma_start(out=rate_sb[:], in_=rate.rearrange("(p t) o -> p (t o)", t=PACK))
         nc.scalar.dma_start(out=off_sb[:], in_=off.rearrange("(p t) o -> p (t o)", t=PACK))
-        nc.scalar.dma_start(out=gap_col[:], in_=gap[0:1, HALF:S].rearrange("o (p c) -> p (o c)", c=2))
-        nc.sync.dma_start(out=gap_lo[:], in_=gap[:, 0:HALF])
+        nc.sync.dma_start(out=gap_col[:], in_=gap[0:1, :].rearrange("o (a p c) -> p (o a) c", a=2, c=2))
         nc.sync.dma_start(offs_sb[:], offs)
         nc.sync.dma_start(out=scales_sb[0:16, :].bitcast(I32), in_=x_scales[0].bitcast(I32))
         nc.sync.dma_start(out=mem_sb[0][:], in_=mem_rows[:, 0, :])
@@ -72,9 +70,10 @@ def tile_picked_ygrud_gate_p_kernel(tc, x_words, x_scales, mem, gap, rate, off, 
 
         ident = keep.tile([P, P], F32, name="ident")
         make_identity(nc, ident[:])
-        gap_ps = psum.tile([P, 2, P], F32, name="gap_ps")
-        for c in range(2):
-            nc.tensor.transpose(gap_ps[:, c, :], gap_col[:, c : c + 1].to_broadcast([P, P]), ident[:])
+        gap_ps = [psum.tile([P, 2, P], F32, name=f"gap_ps{a}") for a in range(2)]
+        for a in range(2):
+            for c in range(2):
+                nc.tensor.transpose(gap_ps[a][:, c, :], gap_col[:, a, c : c + 1].to_broadcast([P, P]), ident[:])
 
         picked_exps = keep.tile([P, S], U8, name="picked_exps")
         nc.vector.tensor_copy(picked_exps[:], scales_sb[:].indirect(offs_sb[:]))
@@ -82,7 +81,7 @@ def tile_picked_ygrud_gate_p_kernel(tc, x_words, x_scales, mem, gap, rate, off, 
             nc.sync.dma_start(
                 out=x_exps[32 * q : 32 * q + 4, :].bitcast(I32), in_=picked_exps[4 * q : 4 * q + 4, :].bitcast(I32)
             )
-        gap_halves = [gap_lo[:].rearrange("q (p c) -> q p c", c=2), gap_ps[:].rearrange("q c p -> q p c")]
+        gap_halves = [gap_ps[a][:].rearrange("q c p -> q p c") for a in range(2)]
 
         h_rows = keep.tile([P, PACK, S], F32, name="h_rows", align_bytes=64)
         for t in range(PACK):
@@ -99,6 +98,9 @@ def tile_picked_ygrud_gate_p_kernel(tc, x_words, x_scales, mem, gap, rate, off, 
             fade = keep.tile([P, S], F32, name=f"fade{t}", align_bytes=64)
             for a in range(2):
                 nc.scalar.activation(fade[:, a * HALF : (a + 1) * HALF], clamped[a][:], ACT.Exp, scale=-1.0)
+            if t == PACK - 1:
+                warm1 = keep.tile([P, 1], F32, name="warm1")
+                nc.scalar.activation(warm1[:], fade[:, S - 1 : S], ACT.Sigmoid)
             for lo, hi in [(0, HALF), (HALF, S)] if t in (0, PACK - 1) else [(0, S)]:
                 nc.vector.tensor_tensor(
                     h_rows[:, t, lo:hi],
@@ -147,8 +149,6 @@ def tile_picked_ygrud_gate_p_kernel(tc, x_words, x_scales, mem, gap, rate, off, 
                 x_codes[:, lo:hi], words_sb[:].bitcast(U32).indirect(offs_sb[:, lo // 16 : hi // 16])
             )
             one_pass(acc[i][:], slice(0, N), x_codes[:, lo:hi], x_exps[:, lo:hi], False)
-            half_tanh = keep.tile([N, hi - lo], F32, name=f"half_tanh{lo}")
-            nc.scalar.activation(half_tanh[:], acc[i][:], ACT.Tanh, scale=0.5)
             gate = keep.tile([N, hi - lo], F32, name=f"gate{lo}")
-            nc.vector.tensor_scalar(gate[:], half_tanh[:], 0.5, 0.5, ALU.mult, ALU.add)
+            nc.scalar.activation(gate[:], acc[i][:], ACT.Sigmoid)
             nc.sync.dma_start(out=out[:, lo:hi], in_=gate[:])

@@ -42,7 +42,7 @@ def tile_picked_ygrud_gate_p_kernel(tc, x_words, x_scales, mem, gap, rate, off, 
         rate_sb = keep.tile([P, PACK], F32, name="rate_sb")
         off_sb = keep.tile([P, PACK], F32, name="off_sb")
         mem_sb = [keep.tile([P, U], F32, name=f"mem_sb{t}") for t in range(PACK)]
-        rr_sb = keep.tile([P, PACK, N], F32, name="rr_sb")
+        rr_sb = keep.tile([P, PACK, N], F32, name="rr_sb", align_bytes=64)
         w1_sb = keep.tile([P, PACK, N], F32, name="w1_sb")
         words_sb = keep.tile([P, T], I32, name="words_sb")
         scales_sb = keep.tile([P, T], U8, name="scales_sb")
@@ -51,16 +51,16 @@ def tile_picked_ygrud_gate_p_kernel(tc, x_words, x_scales, mem, gap, rate, off, 
         nc.vector.memset(scales_sb[:].bitcast(I32), 0)
         nc.vector.memset(x_exps[:].bitcast(I32), 0)
         mem_rows = mem.rearrange("(p t) u -> p t u", t=PACK)
+        nc.scalar.dma_start(out=gap_col[:], in_=gap[0:1, :].rearrange("o (a p c) -> p (o a) c", a=2, c=2))
         nc.scalar.dma_start(out=rate_sb[:], in_=rate.rearrange("(p t) o -> p (t o)", t=PACK))
         nc.scalar.dma_start(out=off_sb[:], in_=off.rearrange("(p t) o -> p (t o)", t=PACK))
-        nc.sync.dma_start(out=gap_col[:], in_=gap[0:1, :].rearrange("o (a p c) -> p (o a) c", a=2, c=2))
         nc.sync.dma_start(offs_sb[:], offs)
         nc.sync.dma_start(out=scales_sb[0:16, :].bitcast(I32), in_=x_scales[0].bitcast(I32))
+        nc.sync.dma_start(out=w1_sb[:], in_=w1.rearrange("(p t) n -> p t n", t=PACK))
         nc.sync.dma_start(out=mem_sb[0][:], in_=mem_rows[:, 0, :])
         nc.sync.dma_start(slot_sb[:], slot)
         for t in range(1, PACK):
             nc.sync.dma_start(out=mem_sb[t][:], in_=mem_rows[:, t, :])
-        nc.sync.dma_start(out=w1_sb[:], in_=w1.rearrange("(p t) n -> p t n", t=PACK))
         nc.sync.dma_start(out=rr_sb[:], in_=rr.rearrange("(p t) n -> p t n", t=PACK))
         nc.sync.dma_start(out=words_sb[:], in_=x_words[0].rearrange("p c r -> p (c r)").bitcast(I32))
 
@@ -83,6 +83,20 @@ def tile_picked_ygrud_gate_p_kernel(tc, x_words, x_scales, mem, gap, rate, off, 
             )
         gap_halves = [gap_ps[a][:].rearrange("q c p -> q p c") for a in range(2)]
 
+        w_codes = keep.tile([P, 2 * N], U32, name="w_codes", align_bytes=64)
+        w_exps = keep.tile([P, 2 * N], U8, name="w_exps", align_bytes=64)
+
+        def quantize_weight(i, w_bf):
+            nc.vector.quantize_mx(
+                out=w_codes[:, i * N : (i + 1) * N].bitcast(FP8X4),
+                scales=w_exps[:, i * N : (i + 1) * N],
+                in_=w_bf[:].rearrange("p n t -> p (n t)"),
+            )
+
+        w1_bf = keep.tile([P, N, PACK], BF16, name="w1_bf", align_bytes=64)
+        interleave(nc.vector.tensor_copy, w1_bf[:], w1_sb[:])
+        quantize_weight(0, w1_bf)
+
         h_rows = keep.tile([P, PACK, S], F32, name="h_rows", align_bytes=64)
         for t in range(PACK):
             clamped = []
@@ -95,28 +109,28 @@ def tile_picked_ygrud_gate_p_kernel(tc, x_words, x_scales, mem, gap, rate, off, 
                     bias=off_sb[:, t : t + 1],
                     scale=rate_sb[:, t : t + 1],
                 )
-            fade = keep.tile([P, S], F32, name=f"fade{t}", align_bytes=64)
+            if t == PACK - 1:
+                halves = [ring.tile([P, HALF], F32, name=f"fade{t}{a}", tag="fade", align_bytes=64) for a in range(2)]
+                halves = [half[:] for half in halves]
+            else:
+                fade = keep.tile([P, S], F32, name=f"fade{t}", align_bytes=64)
+                halves = [fade[:, 0:HALF], fade[:, HALF:S]]
             for a in range(2):
-                nc.scalar.activation(fade[:, a * HALF : (a + 1) * HALF], clamped[a][:], ACT.Exp, scale=-1.0)
+                nc.scalar.activation(halves[a], clamped[a][:], ACT.Exp, scale=-1.0)
             if t == PACK - 1:
                 warm1 = keep.tile([P, 1], F32, name="warm1")
-                nc.scalar.activation(warm1[:], fade[:, S - 1 : S], ACT.Sigmoid)
+                nc.scalar.activation(warm1[:], halves[1][:, 0:1], ACT.Sigmoid)
             for lo, hi in [(0, HALF), (HALF, S)] if t in (0, PACK - 1) else [(0, S)]:
                 nc.vector.tensor_tensor(
                     h_rows[:, t, lo:hi],
                     mem_sb[t][:].indirect(slot_sb[:, lo // 16 : hi // 16]),
-                    fade[:, lo:hi],
+                    halves[lo // HALF] if hi - lo == HALF else fade[:],
                     ALU.mult,
                 )
 
-        w_bf = keep.tile([P, 2 * N, PACK], BF16, name="w_bf", tag="fade3", align_bytes=64)
-        interleave(nc.vector.tensor_copy, w_bf[:, 0:N, :], w1_sb[:])
-        interleave(nc.vector.tensor_copy, w_bf[:, N : 2 * N, :], rr_sb[:])
-        w_codes = keep.tile([P, 2 * N], U32, name="w_codes", align_bytes=64)
-        w_exps = keep.tile([P, 2 * N], U8, name="w_exps", align_bytes=64)
-        nc.vector.quantize_mx(
-            out=w_codes[:].bitcast(FP8X4), scales=w_exps[:], in_=w_bf[:].rearrange("p n t -> p (n t)")
-        )
+        rr_bf = ring.tile([P, N, PACK], BF16, name="rr_bf", tag="fade", align_bytes=64)
+        interleave(nc.vector.tensor_copy, rr_bf[:], rr_sb[:])
+        quantize_weight(1, rr_bf)
 
         h_bf = []
         for lo, hi in PIECES:
@@ -135,20 +149,37 @@ def tile_picked_ygrud_gate_p_kernel(tc, x_words, x_scales, mem, gap, rate, off, 
             )
 
         acc = [psum.tile([N, hi - lo], F32, name=f"acc{lo}") for lo, hi in PIECES]
-        for i, (lo, hi) in enumerate(PIECES):
+        x_codes = [
+            pool.tile([P, hi - lo], U32, name=f"x_codes{lo}", tag=tag, align_bytes=64)
+            for (lo, hi), pool, tag in zip(PIECES, [ring, keep, keep], ["fade", "rr_sb", "h_rows"])
+        ]
+
+        def state_pass(i, first):
+            lo, hi = PIECES[i]
             h_codes = keep.tile([P, hi - lo], U32, name=f"h_codes{lo}", align_bytes=64)
             h_exps = keep.tile([P, hi - lo], U8, name=f"h_exps{lo}", align_bytes=64)
             nc.vector.quantize_mx(
                 out=h_codes[:].bitcast(FP8X4), scales=h_exps[:], in_=h_bf[i][:].rearrange("p j t -> p (j t)")
             )
-            one_pass(acc[i][:], slice(N, 2 * N), h_codes[:], h_exps[:], True)
+            one_pass(acc[i][:], slice(N, 2 * N), h_codes[:], h_exps[:], first)
 
-        x_codes = keep.tile([P, S], U32, name="x_codes", tag="h_rows", align_bytes=64)
-        for i, (lo, hi) in enumerate(PIECES):
-            nc.vector.tensor_copy(
-                x_codes[:, lo:hi], words_sb[:].bitcast(U32).indirect(offs_sb[:, lo // 16 : hi // 16])
-            )
-            one_pass(acc[i][:], slice(0, N), x_codes[:, lo:hi], x_exps[:, lo:hi], False)
+        def input_pass(i, first):
+            lo, hi = PIECES[i]
+            codes = x_codes[i][:]
+            nc.vector.tensor_copy(codes, words_sb[:].bitcast(U32).indirect(offs_sb[:, lo // 16 : hi // 16]))
+            one_pass(acc[i][:], slice(0, N), codes, x_exps[:, lo:hi], first)
+
+        def finish(i):
+            lo, hi = PIECES[i]
             gate = keep.tile([N, hi - lo], F32, name=f"gate{lo}")
             nc.scalar.activation(gate[:], acc[i][:], ACT.Sigmoid)
             nc.sync.dma_start(out=out[:, lo:hi], in_=gate[:])
+
+        for i in (0, 1):
+            input_pass(i, True)
+        for i in (0, 1):
+            state_pass(i, False)
+            finish(i)
+        state_pass(2, True)
+        input_pass(2, False)
+        finish(2)

@@ -34,6 +34,7 @@ def tile_picked_ygrud_gate_p_kernel(tc, x_words, x_scales, mem, gap, rate, off, 
     with ExitStack() as ctx:
         keep = ctx.enter_context(tc.tile_pool(name="keep", bufs=1))
         ring = ctx.enter_context(tc.tile_pool(name="ring", bufs=2))
+        reuse = ctx.enter_context(tc.tile_pool(name="reuse", bufs=1))
         psum = ctx.enter_context(tc.psum_pool(name="psum", bufs=1))
 
         slot_sb = keep.tile([P, S // 16], U16, name="slot_sb")
@@ -42,7 +43,7 @@ def tile_picked_ygrud_gate_p_kernel(tc, x_words, x_scales, mem, gap, rate, off, 
         rate_sb = keep.tile([P, PACK], F32, name="rate_sb")
         off_sb = keep.tile([P, PACK], F32, name="off_sb")
         mem_sb = [keep.tile([P, U], F32, name=f"mem_sb{t}") for t in range(PACK)]
-        rr_sb = keep.tile([P, PACK, N], F32, name="rr_sb", align_bytes=64)
+        rr_sb = reuse.tile([P, PACK, N], F32, name="rr_sb", align_bytes=64, offset=0)
         w1_sb = keep.tile([P, PACK, N], F32, name="w1_sb")
         words_sb = keep.tile([P, T], I32, name="words_sb")
         scales_sb = keep.tile([P, T], U8, name="scales_sb")
@@ -61,11 +62,11 @@ def tile_picked_ygrud_gate_p_kernel(tc, x_words, x_scales, mem, gap, rate, off, 
         nc.sync.dma_start(slot_sb[:], slot)
         for t in range(1, PACK):
             nc.sync.dma_start(out=mem_sb[t][:], in_=mem_rows[:, t, :])
-        nc.sync.dma_start(out=rr_sb[:], in_=rr.rearrange("(p t) n -> p t n", t=PACK))
         nc.sync.dma_start(out=words_sb[:], in_=x_words[0].rearrange("p c r -> p (c r)").bitcast(I32))
+        nc.sync.dma_start(out=rr_sb[:], in_=rr.rearrange("(p t) n -> p t n", t=PACK))
 
         warm = keep.tile([P, 1], F32, name="warm")
-        nc.gpsimd.memset(warm[:], 0.0)
+        nc.vector.memset(warm[:], 0.0)
         nc.scalar.activation(warm[:], warm[:], ACT.Exp)
 
         ident = keep.tile([P, P], F32, name="ident")
@@ -83,13 +84,13 @@ def tile_picked_ygrud_gate_p_kernel(tc, x_words, x_scales, mem, gap, rate, off, 
             )
         gap_halves = [gap_ps[a][:].rearrange("q c p -> q p c") for a in range(2)]
 
-        w_codes = keep.tile([P, 2 * N], U32, name="w_codes", align_bytes=64)
-        w_exps = keep.tile([P, 2 * N], U8, name="w_exps", align_bytes=64)
+        w_codes = [keep.tile([P, N], U32, name=f"w_codes{i}", align_bytes=64) for i in range(2)]
+        w_exps = [keep.tile([P, N], U8, name=f"w_exps{i}", align_bytes=64) for i in range(2)]
 
         def quantize_weight(i, w_bf):
             nc.vector.quantize_mx(
-                out=w_codes[:, i * N : (i + 1) * N].bitcast(FP8X4),
-                scales=w_exps[:, i * N : (i + 1) * N],
+                out=w_codes[i][:].bitcast(FP8X4),
+                scales=w_exps[i][:],
                 in_=w_bf[:].rearrange("p n t -> p (n t)"),
             )
 
@@ -109,39 +110,30 @@ def tile_picked_ygrud_gate_p_kernel(tc, x_words, x_scales, mem, gap, rate, off, 
                     bias=off_sb[:, t : t + 1],
                     scale=rate_sb[:, t : t + 1],
                 )
-            if t == PACK - 1:
-                halves = [ring.tile([P, HALF], F32, name=f"fade{t}{a}", tag="fade", align_bytes=64) for a in range(2)]
-                halves = [half[:] for half in halves]
-            else:
-                fade = keep.tile([P, S], F32, name=f"fade{t}", align_bytes=64)
-                halves = [fade[:, 0:HALF], fade[:, HALF:S]]
+            fade = keep.tile([P, S], F32, name=f"fade{t}")
             for a in range(2):
-                nc.scalar.activation(halves[a], clamped[a][:], ACT.Exp, scale=-1.0)
+                nc.scalar.activation(fade[:, a * HALF : (a + 1) * HALF], clamped[a][:], ACT.Exp, scale=-1.0)
             if t == PACK - 1:
-                warm1 = keep.tile([P, 1], F32, name="warm1")
-                nc.scalar.activation(warm1[:], halves[1][:, 0:1], ACT.Sigmoid)
+                warm1 = reuse.tile([P, 640], F32, name="warm1", align_bytes=64, offset=2048)
+                nc.scalar.activation(warm1[:, 0:1], fade[:, S - 1 : S], ACT.Sigmoid)
             for lo, hi in [(0, HALF), (HALF, S)] if t in (0, PACK - 1) else [(0, S)]:
                 nc.vector.tensor_tensor(
                     h_rows[:, t, lo:hi],
                     mem_sb[t][:].indirect(slot_sb[:, lo // 16 : hi // 16]),
-                    halves[lo // HALF] if hi - lo == HALF else fade[:],
+                    fade[:, lo:hi],
                     ALU.mult,
                 )
-
-        rr_bf = ring.tile([P, N, PACK], BF16, name="rr_bf", tag="fade", align_bytes=64)
-        interleave(nc.vector.tensor_copy, rr_bf[:], rr_sb[:])
-        quantize_weight(1, rr_bf)
 
         h_bf = []
         for lo, hi in PIECES:
             h_bf.append(keep.tile([P, hi - lo, PACK], BF16, name=f"h_bf{lo}", align_bytes=64))
             interleave(nc.scalar.copy, h_bf[-1][:], h_rows[:, :, lo:hi])
 
-        def one_pass(acc, w_cols, codes, exps, first):
+        def one_pass(acc, w, codes, exps, first):
             nc.tensor.matmul_mx(
                 out=acc,
-                lhsT=w_codes[:, w_cols].bitcast(FP8X4),
-                lhsT_scale=w_exps[:, w_cols],
+                lhsT=w_codes[w][:].bitcast(FP8X4),
+                lhsT_scale=w_exps[w][:],
                 rhs=codes.bitcast(FP8X4),
                 rhs_scale=exps,
                 start=first,
@@ -149,25 +141,27 @@ def tile_picked_ygrud_gate_p_kernel(tc, x_words, x_scales, mem, gap, rate, off, 
             )
 
         acc = [psum.tile([N, hi - lo], F32, name=f"acc{lo}") for lo, hi in PIECES]
+        rr_bf = reuse.tile([P, N, PACK], BF16, name="rr_bf", align_bytes=64, offset=3072)
         x_codes = [
-            pool.tile([P, hi - lo], U32, name=f"x_codes{lo}", tag=tag, align_bytes=64)
-            for (lo, hi), pool, tag in zip(PIECES, [ring, keep, keep], ["fade", "rr_sb", "h_rows"])
+            reuse.tile([P, HALF], U32, name="x_codes0", align_bytes=64, offset=2048),
+            reuse.tile([P, P], U32, name="x_codes1", align_bytes=64, offset=4096),
+            keep.tile([P, P], U32, name="x_codes2", tag="h_rows", align_bytes=64),
         ]
 
         def state_pass(i, first):
             lo, hi = PIECES[i]
             h_codes = keep.tile([P, hi - lo], U32, name=f"h_codes{lo}", align_bytes=64)
-            h_exps = keep.tile([P, hi - lo], U8, name=f"h_exps{lo}", align_bytes=64)
+            h_exps = reuse.tile([P, hi - lo], U8, name=f"h_exps{lo}", align_bytes=64, offset=lo)
             nc.vector.quantize_mx(
                 out=h_codes[:].bitcast(FP8X4), scales=h_exps[:], in_=h_bf[i][:].rearrange("p j t -> p (j t)")
             )
-            one_pass(acc[i][:], slice(N, 2 * N), h_codes[:], h_exps[:], first)
+            one_pass(acc[i][:], 1, h_codes[:], h_exps[:], first)
 
         def input_pass(i, first):
             lo, hi = PIECES[i]
             codes = x_codes[i][:]
             nc.vector.tensor_copy(codes, words_sb[:].bitcast(U32).indirect(offs_sb[:, lo // 16 : hi // 16]))
-            one_pass(acc[i][:], slice(0, N), codes, x_exps[:, lo:hi], first)
+            one_pass(acc[i][:], 0, codes, x_exps[:, lo:hi], first)
 
         def finish(i):
             lo, hi = PIECES[i]
@@ -175,8 +169,10 @@ def tile_picked_ygrud_gate_p_kernel(tc, x_words, x_scales, mem, gap, rate, off, 
             nc.scalar.activation(gate[:], acc[i][:], ACT.Sigmoid)
             nc.sync.dma_start(out=out[:, lo:hi], in_=gate[:])
 
-        for i in (0, 1):
-            input_pass(i, True)
+        input_pass(0, True)
+        interleave(nc.vector.tensor_copy, rr_bf[:], rr_sb[:])
+        input_pass(1, True)
+        quantize_weight(1, rr_bf)
         for i in (0, 1):
             state_pass(i, False)
             finish(i)

@@ -49,7 +49,7 @@ def tile_picked_ygrud_gate_p_kernel(tc, x_words, x_scales, mem, gap, rate, off, 
         scales_sb = keep.tile([P, T], U8, name="scales_sb")
         x_exps = keep.tile([P, S], U8, name="x_exps", align_bytes=64)
 
-        nc.vector.memset(scales_sb[:].bitcast(I32), 0)
+        nc.gpsimd.memset(scales_sb[:].bitcast(I32), 0)
         nc.vector.memset(x_exps[:].bitcast(I32), 0)
         mem_rows = mem.rearrange("(p t) u -> p t u", t=PACK)
         nc.scalar.dma_start(out=gap_col[:], in_=gap[0:1, :].rearrange("o (a p c) -> p (o a) c", a=2, c=2))
@@ -116,13 +116,7 @@ def tile_picked_ygrud_gate_p_kernel(tc, x_words, x_scales, mem, gap, rate, off, 
             if t == PACK - 1:
                 warm1 = reuse.tile([P, 640], F32, name="warm1", align_bytes=64, offset=2048)
                 nc.scalar.activation(warm1[:, 0:1], fade[:, S - 1 : S], ACT.Sigmoid)
-            for lo, hi in [(0, HALF), (HALF, S)] if t in (0, PACK - 1) else [(0, S)]:
-                nc.vector.tensor_tensor(
-                    h_rows[:, t, lo:hi],
-                    mem_sb[t][:].indirect(slot_sb[:, lo // 16 : hi // 16]),
-                    fade[:, lo:hi],
-                    ALU.mult,
-                )
+            nc.vector.tensor_tensor(h_rows[:, t, :], mem_sb[t][:].indirect(slot_sb[:]), fade[:], ALU.mult)
 
         h_bf = []
         for lo, hi in PIECES:
@@ -145,7 +139,7 @@ def tile_picked_ygrud_gate_p_kernel(tc, x_words, x_scales, mem, gap, rate, off, 
         x_codes = [
             reuse.tile([P, HALF], U32, name="x_codes0", align_bytes=64, offset=2048),
             reuse.tile([P, P], U32, name="x_codes1", align_bytes=64, offset=4096),
-            keep.tile([P, P], U32, name="x_codes2", tag="h_rows", align_bytes=64),
+            keep.tile([P, P], U32, name="x_codes2", tag="h_bf0", align_bytes=64),
         ]
 
         def state_pass(i, first):
@@ -173,9 +167,9 @@ def tile_picked_ygrud_gate_p_kernel(tc, x_words, x_scales, mem, gap, rate, off, 
         interleave(nc.vector.tensor_copy, rr_bf[:], rr_sb[:])
         input_pass(1, True)
         quantize_weight(1, rr_bf)
-        for i in (0, 1):
+        state_pass(0, False)
+        finish(0)
+        input_pass(2, True)
+        for i in (1, 2):
             state_pass(i, False)
             finish(i)
-        state_pass(2, True)
-        input_pass(2, False)
-        finish(2)

@@ -49,7 +49,7 @@ def tile_picked_ygrud_gate_p_kernel(tc, x_words, x_scales, mem, gap, rate, off, 
         scales_sb = keep.tile([P, T], U8, name="scales_sb")
         x_exps = keep.tile([P, S], U8, name="x_exps", align_bytes=64)
 
-        nc.gpsimd.memset(scales_sb[:].bitcast(I32), 0)
+        nc.vector.memset(scales_sb[:].bitcast(I32), 0)
         nc.vector.memset(x_exps[:].bitcast(I32), 0)
         mem_rows = mem.rearrange("(p t) u -> p t u", t=PACK)
         nc.scalar.dma_start(out=gap_col[:], in_=gap[0:1, :].rearrange("o (a p c) -> p (o a) c", a=2, c=2))

@@ -20,6 +20,13 @@ P = 128
 PACK = 4
 HALF = S // 2
 PIECES = [(0, 256), (256, 384), (384, 512)]
+W1, RR = 0, 1
+
+RR_AT = 0
+X_CODES0_AT = 2048
+X_CODES1_AT = 3072
+RR_BF_AT = 3584
+LAST_CLAMPED_AT = (4608, 2816)
 
 
 def interleave(copy, dst, src):
@@ -43,7 +50,7 @@ def tile_picked_ygrud_gate_p_kernel(tc, x_words, x_scales, mem, gap, rate, off, 
         rate_sb = keep.tile([P, PACK], F32, name="rate_sb")
         off_sb = keep.tile([P, PACK], F32, name="off_sb")
         mem_sb = [keep.tile([P, U], F32, name=f"mem_sb{t}") for t in range(PACK)]
-        rr_sb = reuse.tile([P, PACK, N], F32, name="rr_sb", align_bytes=64, offset=0)
+        rr_sb = reuse.tile([P, PACK, N], F32, name="rr_sb", align_bytes=64, offset=RR_AT)
         w1_sb = keep.tile([P, PACK, N], F32, name="w1_sb")
         words_sb = keep.tile([P, T], I32, name="words_sb")
         scales_sb = keep.tile([P, T], U8, name="scales_sb")
@@ -51,8 +58,9 @@ def tile_picked_ygrud_gate_p_kernel(tc, x_words, x_scales, mem, gap, rate, off, 
 
         nc.vector.memset(scales_sb[:].bitcast(I32), 0)
         nc.vector.memset(x_exps[:].bitcast(I32), 0)
+
         mem_rows = mem.rearrange("(p t) u -> p t u", t=PACK)
-        nc.scalar.dma_start(out=gap_col[:], in_=gap[0:1, :].rearrange("o (a p c) -> p (o a) c", a=2, c=2))
+        nc.sync.dma_start(out=gap_col[:], in_=gap[0:1, :].rearrange("o (a p c) -> p (o a) c", a=2, c=2))
         nc.scalar.dma_start(out=rate_sb[:], in_=rate.rearrange("(p t) o -> p (t o)", t=PACK))
         nc.scalar.dma_start(out=off_sb[:], in_=off.rearrange("(p t) o -> p (t o)", t=PACK))
         nc.sync.dma_start(offs_sb[:], offs)
@@ -65,9 +73,9 @@ def tile_picked_ygrud_gate_p_kernel(tc, x_words, x_scales, mem, gap, rate, off, 
         nc.sync.dma_start(out=words_sb[:], in_=x_words[0].rearrange("p c r -> p (c r)").bitcast(I32))
         nc.sync.dma_start(out=rr_sb[:], in_=rr.rearrange("(p t) n -> p t n", t=PACK))
 
-        warm = keep.tile([P, 1], F32, name="warm")
-        nc.vector.memset(warm[:], 0.0)
-        nc.scalar.activation(warm[:], warm[:], ACT.Exp)
+        exp_warm = keep.tile([P, 1], F32, name="exp_warm")
+        nc.vector.memset(exp_warm[:], 0.0)
+        nc.scalar.activation(exp_warm[:], exp_warm[:], ACT.Exp)
 
         ident = keep.tile([P, P], F32, name="ident")
         make_identity(nc, ident[:])
@@ -84,25 +92,31 @@ def tile_picked_ygrud_gate_p_kernel(tc, x_words, x_scales, mem, gap, rate, off, 
             )
         gap_halves = [gap_ps[a][:].rearrange("q c p -> q p c") for a in range(2)]
 
-        w_codes = [keep.tile([P, N], U32, name=f"w_codes{i}", align_bytes=64) for i in range(2)]
-        w_exps = [keep.tile([P, N], U8, name=f"w_exps{i}", align_bytes=64) for i in range(2)]
+        w_codes = [keep.tile([P, N], U32, name=f"w_codes{w}", align_bytes=64) for w in (W1, RR)]
+        w_exps = [keep.tile([P, N], U8, name=f"w_exps{w}", align_bytes=64) for w in (W1, RR)]
 
-        def quantize_weight(i, w_bf):
+        def quantize_weight(w, w_bf):
             nc.vector.quantize_mx(
-                out=w_codes[i][:].bitcast(FP8X4),
-                scales=w_exps[i][:],
+                out=w_codes[w][:].bitcast(FP8X4),
+                scales=w_exps[w][:],
                 in_=w_bf[:].rearrange("p n t -> p (n t)"),
             )
 
         w1_bf = keep.tile([P, N, PACK], BF16, name="w1_bf", align_bytes=64)
         interleave(nc.vector.tensor_copy, w1_bf[:], w1_sb[:])
-        quantize_weight(0, w1_bf)
+        quantize_weight(W1, w1_bf)
 
         h_rows = keep.tile([P, PACK, S], F32, name="h_rows", align_bytes=64)
         for t in range(PACK):
+            last_plane = t == PACK - 1
             clamped = []
             for a in range(2):
-                clamped.append(ring.tile([P, HALF], F32, name="clamped"))
+                if last_plane:
+                    clamped.append(
+                        reuse.tile([P, HALF], F32, name=f"last_clamped{a}", align_bytes=64, offset=LAST_CLAMPED_AT[a])
+                    )
+                else:
+                    clamped.append(ring.tile([P, HALF], F32, name="clamped"))
                 nc.scalar.activation(
                     clamped[a][:].rearrange("q (p c) -> q p c", c=2),
                     gap_halves[a],
@@ -113,19 +127,24 @@ def tile_picked_ygrud_gate_p_kernel(tc, x_words, x_scales, mem, gap, rate, off, 
             fade = keep.tile([P, S], F32, name=f"fade{t}")
             for a in range(2):
                 nc.scalar.activation(fade[:, a * HALF : (a + 1) * HALF], clamped[a][:], ACT.Exp, scale=-1.0)
-            if t == PACK - 1:
-                warm1 = reuse.tile([P, 640], F32, name="warm1", align_bytes=64, offset=2048)
-                nc.scalar.activation(warm1[:, 0:1], fade[:, S - 1 : S], ACT.Sigmoid)
-            nc.vector.tensor_tensor(h_rows[:, t, :], mem_sb[t][:].indirect(slot_sb[:]), fade[:], ALU.mult)
+            if last_plane:
+                nc.scalar.activation(clamped[1][:, 0:1], fade[:, S - 1 : S], ACT.Sigmoid)
+            for lo, hi in [(0, HALF), (HALF, S)] if t == 0 or last_plane else [(0, S)]:
+                nc.vector.tensor_tensor(
+                    h_rows[:, t, lo:hi],
+                    mem_sb[t][:].indirect(slot_sb[:, lo // 16 : hi // 16]),
+                    fade[:, lo:hi],
+                    ALU.mult,
+                )
 
         h_bf = []
         for lo, hi in PIECES:
             h_bf.append(keep.tile([P, hi - lo, PACK], BF16, name=f"h_bf{lo}", align_bytes=64))
             interleave(nc.scalar.copy, h_bf[-1][:], h_rows[:, :, lo:hi])
 
-        def one_pass(acc, w, codes, exps, first):
+        def one_pass(group, w, codes, exps, first):
             nc.tensor.matmul_mx(
-                out=acc,
+                out=group,
                 lhsT=w_codes[w][:].bitcast(FP8X4),
                 lhsT_scale=w_exps[w][:],
                 rhs=codes.bitcast(FP8X4),
@@ -135,27 +154,27 @@ def tile_picked_ygrud_gate_p_kernel(tc, x_words, x_scales, mem, gap, rate, off, 
             )
 
         acc = [psum.tile([N, hi - lo], F32, name=f"acc{lo}") for lo, hi in PIECES]
-        rr_bf = reuse.tile([P, N, PACK], BF16, name="rr_bf", align_bytes=64, offset=3072)
+        rr_bf = reuse.tile([P, N, PACK], BF16, name="rr_bf", align_bytes=64, offset=RR_BF_AT)
         x_codes = [
-            reuse.tile([P, HALF], U32, name="x_codes0", align_bytes=64, offset=2048),
-            reuse.tile([P, P], U32, name="x_codes1", align_bytes=64, offset=4096),
+            reuse.tile([P, HALF], U32, name="x_codes0", align_bytes=64, offset=X_CODES0_AT),
+            reuse.tile([P, P], U32, name="x_codes1", align_bytes=64, offset=X_CODES1_AT),
             keep.tile([P, P], U32, name="x_codes2", tag="h_bf0", align_bytes=64),
         ]
 
         def state_pass(i, first):
             lo, hi = PIECES[i]
             h_codes = keep.tile([P, hi - lo], U32, name=f"h_codes{lo}", align_bytes=64)
-            h_exps = reuse.tile([P, hi - lo], U8, name=f"h_exps{lo}", align_bytes=64, offset=lo)
+            h_exps = reuse.tile([P, hi - lo], U8, name=f"h_exps{lo}", align_bytes=64, offset=RR_AT + lo)
             nc.vector.quantize_mx(
                 out=h_codes[:].bitcast(FP8X4), scales=h_exps[:], in_=h_bf[i][:].rearrange("p j t -> p (j t)")
             )
-            one_pass(acc[i][:], 1, h_codes[:], h_exps[:], first)
+            one_pass(acc[i][:], RR, h_codes[:], h_exps[:], first)
 
         def input_pass(i, first):
             lo, hi = PIECES[i]
             codes = x_codes[i][:]
             nc.vector.tensor_copy(codes, words_sb[:].bitcast(U32).indirect(offs_sb[:, lo // 16 : hi // 16]))
-            one_pass(acc[i][:], 0, codes, x_exps[:, lo:hi], first)
+            one_pass(acc[i][:], W1, codes, x_exps[:, lo:hi], first)
 
         def finish(i):
             lo, hi = PIECES[i]
@@ -166,7 +185,7 @@ def tile_picked_ygrud_gate_p_kernel(tc, x_words, x_scales, mem, gap, rate, off, 
         input_pass(0, True)
         interleave(nc.vector.tensor_copy, rr_bf[:], rr_sb[:])
         input_pass(1, True)
-        quantize_weight(1, rr_bf)
+        quantize_weight(RR, rr_bf)
         state_pass(0, False)
         finish(0)
         input_pass(2, True)

@@ -26,13 +26,13 @@ RR_AT = 0
 X_CODES0_AT = 2048
 X_CODES1_AT = 3072
 RR_BF_AT = 3584
-LAST_CLAMPED_AT = (4608, 2816)
+LAST_FADE_AT = 2816
 
 
 def interleave(copy, dst, src):
     copy(
-        out=dst.rearrange("p (c i) t -> p c t i", i=4),
-        in_=src.rearrange("p t (c i) -> p c t i", i=4),
+        out=dst.rearrange("p (c i) t -> p c t i", i=2),
+        in_=src.rearrange("p t (c i) -> p c t i", i=2),
     )
 
 
@@ -46,7 +46,7 @@ def tile_picked_ygrud_gate_p_kernel(tc, x_words, x_scales, mem, gap, rate, off, 
 
         slot_sb = keep.tile([P, S // 16], U16, name="slot_sb")
         offs_sb = keep.tile([P, S // 16], U16, name="offs_sb")
-        gap_col = keep.tile([P, 2, 2], F32, name="gap_col")
+        gap_col = keep.tile([P, 2, 8], F32, name="gap_col")
         rate_sb = keep.tile([P, PACK], F32, name="rate_sb")
         off_sb = keep.tile([P, PACK], F32, name="off_sb")
         mem_sb = [keep.tile([P, U], F32, name=f"mem_sb{t}") for t in range(PACK)]
@@ -60,7 +60,7 @@ def tile_picked_ygrud_gate_p_kernel(tc, x_words, x_scales, mem, gap, rate, off, 
         nc.vector.memset(x_exps[:].bitcast(I32), 0)
 
         mem_rows = mem.rearrange("(p t) u -> p t u", t=PACK)
-        nc.sync.dma_start(out=gap_col[:], in_=gap[0:1, :].rearrange("o (a p c) -> p (o a) c", a=2, c=2))
+        nc.sync.dma_start(out=gap_col[:, :, 0:2], in_=gap[0:1, :].rearrange("o (a p c) -> p (o a) c", a=2, c=2))
         nc.scalar.dma_start(out=rate_sb[:], in_=rate.rearrange("(p t) o -> p (t o)", t=PACK))
         nc.scalar.dma_start(out=off_sb[:], in_=off.rearrange("(p t) o -> p (t o)", t=PACK))
         nc.sync.dma_start(offs_sb[:], offs)
@@ -112,9 +112,7 @@ def tile_picked_ygrud_gate_p_kernel(tc, x_words, x_scales, mem, gap, rate, off, 
             clamped = []
             for a in range(2):
                 if last_plane:
-                    clamped.append(
-                        reuse.tile([P, HALF], F32, name=f"last_clamped{a}", align_bytes=64, offset=LAST_CLAMPED_AT[a])
-                    )
+                    clamped.append(keep.tile([P, HALF], F32, name=f"last_clamped{a}"))
                 else:
                     clamped.append(ring.tile([P, HALF], F32, name="clamped"))
                 nc.scalar.activation(
@@ -124,16 +122,24 @@ def tile_picked_ygrud_gate_p_kernel(tc, x_words, x_scales, mem, gap, rate, off, 
                     bias=off_sb[:, t : t + 1],
                     scale=rate_sb[:, t : t + 1],
                 )
-            fade = keep.tile([P, S], F32, name=f"fade{t}")
-            for a in range(2):
-                nc.scalar.activation(fade[:, a * HALF : (a + 1) * HALF], clamped[a][:], ACT.Exp, scale=-1.0)
             if last_plane:
-                nc.scalar.activation(clamped[1][:, 0:1], fade[:, S - 1 : S], ACT.Sigmoid)
+                fade = [
+                    reuse.tile([P, HALF], F32, name="last_fade0", align_bytes=64, offset=LAST_FADE_AT)[:],
+                    keep.tile([P, HALF], F32, name="last_fade1")[:],
+                ]
+            else:
+                fade_whole = keep.tile([P, S], F32, name=f"fade{t}")
+                fade = [fade_whole[:, 0:HALF], fade_whole[:, HALF:S]]
+            for a in range(2):
+                nc.scalar.activation(fade[a], clamped[a][:], ACT.Exp, scale=-1.0)
+            if last_plane:
+                sigmoid_warm = keep.tile([P, 1], F32, name="sigmoid_warm")
+                nc.scalar.activation(sigmoid_warm[:], fade[1][:, HALF - 1 : HALF], ACT.Sigmoid)
             for lo, hi in [(0, HALF), (HALF, S)] if t == 0 or last_plane else [(0, S)]:
                 nc.vector.tensor_tensor(
                     h_rows[:, t, lo:hi],
                     mem_sb[t][:].indirect(slot_sb[:, lo // 16 : hi // 16]),
-                    fade[:, lo:hi],
+                    fade[lo // HALF] if hi - lo == HALF else fade_whole[:],
                     ALU.mult,
                 )
 
@@ -180,7 +186,8 @@ def tile_picked_ygrud_gate_p_kernel(tc, x_words, x_scales, mem, gap, rate, off, 
             lo, hi = PIECES[i]
             gate = keep.tile([N, hi - lo], F32, name=f"gate{lo}")
             nc.scalar.activation(gate[:], acc[i][:], ACT.Sigmoid)
-            nc.sync.dma_start(out=out[:, lo:hi], in_=gate[:])
+            queue = nc.scalar if hi == S else nc.sync
+            queue.dma_start(out=out[:, lo:hi], in_=gate[:])
 
         input_pass(0, True)
         interleave(nc.vector.tensor_copy, rr_bf[:], rr_sb[:])

@@ -56,7 +56,10 @@ def tile_picked_ygrud_gate_p_kernel(tc, x_words, x_scales, mem, gap, rate, off, 
         scales_sb = keep.tile([P, T], U8, name="scales_sb")
         x_exps = keep.tile([P, S], U8, name="x_exps", align_bytes=64)
 
-        nc.vector.memset(scales_sb[:].bitcast(I32), 0)
+        exp_warm = keep.tile([P, 1], F32, name="exp_warm")
+        nc.vector.memset(exp_warm[:], 0.0)
+        for first, last in [(0, 16), (32, 64), (64, P)]:
+            nc.vector.memset(scales_sb[first:last, :].bitcast(I32), 0)
         nc.vector.memset(x_exps[:].bitcast(I32), 0)
 
         mem_rows = mem.rearrange("(p t) u -> p t u", t=PACK)
@@ -64,7 +67,7 @@ def tile_picked_ygrud_gate_p_kernel(tc, x_words, x_scales, mem, gap, rate, off, 
         nc.scalar.dma_start(out=rate_sb[:], in_=rate.rearrange("(p t) o -> p (t o)", t=PACK))
         nc.scalar.dma_start(out=off_sb[:], in_=off.rearrange("(p t) o -> p (t o)", t=PACK))
         nc.sync.dma_start(offs_sb[:], offs)
-        nc.sync.dma_start(out=scales_sb[0:16, :].bitcast(I32), in_=x_scales[0].bitcast(I32))
+        nc.sync.dma_start(out=scales_sb[16:32, :].bitcast(I32), in_=x_scales[0].bitcast(I32))
         nc.sync.dma_start(out=w1_sb[:], in_=w1.rearrange("(p t) n -> p t n", t=PACK))
         nc.sync.dma_start(out=mem_sb[0][:], in_=mem_rows[:, 0, :])
         nc.sync.dma_start(slot_sb[:], slot)
@@ -73,8 +76,6 @@ def tile_picked_ygrud_gate_p_kernel(tc, x_words, x_scales, mem, gap, rate, off, 
         nc.sync.dma_start(out=words_sb[:], in_=x_words[0].rearrange("p c r -> p (c r)").bitcast(I32))
         nc.sync.dma_start(out=rr_sb[:], in_=rr.rearrange("(p t) n -> p t n", t=PACK))
 
-        exp_warm = keep.tile([P, 1], F32, name="exp_warm")
-        nc.vector.memset(exp_warm[:], 0.0)
         nc.scalar.activation(exp_warm[:], exp_warm[:], ACT.Exp)
 
         ident = keep.tile([P, P], F32, name="ident")
@@ -88,7 +89,7 @@ def tile_picked_ygrud_gate_p_kernel(tc, x_words, x_scales, mem, gap, rate, off, 
         nc.vector.tensor_copy(picked_exps[:], scales_sb[:].indirect(offs_sb[:]))
         for q in range(4):
             nc.sync.dma_start(
-                out=x_exps[32 * q : 32 * q + 4, :].bitcast(I32), in_=picked_exps[4 * q : 4 * q + 4, :].bitcast(I32)
+                out=x_exps[32 * q : 32 * q + 4, :].bitcast(I32), in_=picked_exps[16 + 4 * q : 20 + 4 * q, :].bitcast(I32)
             )
         gap_halves = [gap_ps[a][:].rearrange("q c p -> q p c") for a in range(2)]
 
@@ -135,7 +136,7 @@ def tile_picked_ygrud_gate_p_kernel(tc, x_words, x_scales, mem, gap, rate, off, 
             if last_plane:
                 sigmoid_warm = keep.tile([P, 1], F32, name="sigmoid_warm")
                 nc.scalar.activation(sigmoid_warm[:], fade[1][:, HALF - 1 : HALF], ACT.Sigmoid)
-            for lo, hi in [(0, HALF), (HALF, S)] if t == 0 or last_plane else [(0, S)]:
+            for lo, hi in [(0, HALF), (HALF, S)] if t != 2 else [(0, S)]:
                 nc.vector.tensor_tensor(
                     h_rows[:, t, lo:hi],
                     mem_sb[t][:].indirect(slot_sb[:, lo // 16 : hi // 16]),

@@ -19,14 +19,15 @@ ACT = mybir.ActivationFunctionType
 P = 128
 PACK = 4
 HALF = S // 2
+HALVES = [(0, HALF), (HALF, S)]
 PIECES = [(0, 256), (256, 384), (384, 512)]
 W1, RR = 0, 1
+SCALE_ROWS_AT = 16
 
-RR_AT = 0
-X_CODES0_AT = 2048
-X_CODES1_AT = 3072
-RR_BF_AT = 3584
-LAST_FADE_AT = 2816
+X_CODES_AT = 0
+RR_BF_AT = 2048
+LAST_FADE_AT = 1536
+H_FIRST_AT = 3072
 
 
 def interleave(copy, dst, src):
@@ -50,15 +51,15 @@ def tile_picked_ygrud_gate_p_kernel(tc, x_words, x_scales, mem, gap, rate, off, 
         rate_sb = keep.tile([P, PACK], F32, name="rate_sb")
         off_sb = keep.tile([P, PACK], F32, name="off_sb")
         mem_sb = [keep.tile([P, U], F32, name=f"mem_sb{t}") for t in range(PACK)]
-        rr_sb = reuse.tile([P, PACK, N], F32, name="rr_sb", align_bytes=64, offset=RR_AT)
-        w1_sb = keep.tile([P, PACK, N], F32, name="w1_sb")
+        w1_sb = keep.tile([P, PACK, N], F32, name="w1_sb", tag="weight")
+        rr_sb = keep.tile([P, PACK, N], F32, name="rr_sb", tag="weight")
         words_sb = keep.tile([P, T], I32, name="words_sb")
         scales_sb = keep.tile([P, T], U8, name="scales_sb")
         x_exps = keep.tile([P, S], U8, name="x_exps", align_bytes=64)
 
         exp_warm = keep.tile([P, 1], F32, name="exp_warm")
         nc.vector.memset(exp_warm[:], 0.0)
-        for first, last in [(0, 16), (32, 64), (64, P)]:
+        for first, last in [(0, SCALE_ROWS_AT), (32, 64), (64, P)]:
             nc.vector.memset(scales_sb[first:last, :].bitcast(I32), 0)
         nc.vector.memset(x_exps[:].bitcast(I32), 0)
 
@@ -67,14 +68,13 @@ def tile_picked_ygrud_gate_p_kernel(tc, x_words, x_scales, mem, gap, rate, off, 
         nc.scalar.dma_start(out=rate_sb[:], in_=rate.rearrange("(p t) o -> p (t o)", t=PACK))
         nc.scalar.dma_start(out=off_sb[:], in_=off.rearrange("(p t) o -> p (t o)", t=PACK))
         nc.sync.dma_start(offs_sb[:], offs)
-        nc.sync.dma_start(out=scales_sb[16:32, :].bitcast(I32), in_=x_scales[0].bitcast(I32))
+        nc.sync.dma_start(out=scales_sb[SCALE_ROWS_AT:32, :].bitcast(I32), in_=x_scales[0].bitcast(I32))
         nc.sync.dma_start(out=w1_sb[:], in_=w1.rearrange("(p t) n -> p t n", t=PACK))
         nc.sync.dma_start(out=mem_sb[0][:], in_=mem_rows[:, 0, :])
         nc.sync.dma_start(slot_sb[:], slot)
         for t in range(1, PACK):
             nc.sync.dma_start(out=mem_sb[t][:], in_=mem_rows[:, t, :])
         nc.sync.dma_start(out=words_sb[:], in_=x_words[0].rearrange("p c r -> p (c r)").bitcast(I32))
-        nc.sync.dma_start(out=rr_sb[:], in_=rr.rearrange("(p t) n -> p t n", t=PACK))
 
         nc.scalar.activation(exp_warm[:], exp_warm[:], ACT.Exp)
 
@@ -88,13 +88,17 @@ def tile_picked_ygrud_gate_p_kernel(tc, x_words, x_scales, mem, gap, rate, off, 
         picked_exps = keep.tile([P, S], U8, name="picked_exps")
         nc.vector.tensor_copy(picked_exps[:], scales_sb[:].indirect(offs_sb[:]))
         for q in range(4):
+            row = SCALE_ROWS_AT + 4 * q
             nc.sync.dma_start(
-                out=x_exps[32 * q : 32 * q + 4, :].bitcast(I32), in_=picked_exps[16 + 4 * q : 20 + 4 * q, :].bitcast(I32)
+                out=x_exps[32 * q : 32 * q + 4, :].bitcast(I32), in_=picked_exps[row : row + 4, :].bitcast(I32)
             )
         gap_halves = [gap_ps[a][:].rearrange("q c p -> q p c") for a in range(2)]
 
         w_codes = [keep.tile([P, N], U32, name=f"w_codes{w}", align_bytes=64) for w in (W1, RR)]
-        w_exps = [keep.tile([P, N], U8, name=f"w_exps{w}", align_bytes=64) for w in (W1, RR)]
+        w_exps = [
+            keep.tile([P, N], U8, name="w1_exps", align_bytes=64),
+            reuse.tile([P, N], U8, name="rr_exps", align_bytes=64, offset=H_FIRST_AT),
+        ]
 
         def quantize_weight(w, w_bf):
             nc.vector.quantize_mx(
@@ -106,8 +110,12 @@ def tile_picked_ygrud_gate_p_kernel(tc, x_words, x_scales, mem, gap, rate, off, 
         w1_bf = keep.tile([P, N, PACK], BF16, name="w1_bf", align_bytes=64)
         interleave(nc.vector.tensor_copy, w1_bf[:], w1_sb[:])
         quantize_weight(W1, w1_bf)
+        nc.sync.dma_start(out=rr_sb[:], in_=rr.rearrange("(p t) n -> p t n", t=PACK))
 
-        h_rows = keep.tile([P, PACK, S], F32, name="h_rows", align_bytes=64)
+        h_rows = [
+            reuse.tile([P, PACK, HALF], F32, name="h_rows0", align_bytes=64, offset=H_FIRST_AT),
+            keep.tile([P, PACK, HALF], F32, name="h_rows1", align_bytes=64),
+        ]
         for t in range(PACK):
             last_plane = t == PACK - 1
             clamped = []
@@ -136,18 +144,15 @@ def tile_picked_ygrud_gate_p_kernel(tc, x_words, x_scales, mem, gap, rate, off, 
             if last_plane:
                 sigmoid_warm = keep.tile([P, 1], F32, name="sigmoid_warm")
                 nc.scalar.activation(sigmoid_warm[:], fade[1][:, HALF - 1 : HALF], ACT.Sigmoid)
-            for lo, hi in [(0, HALF), (HALF, S)] if t != 2 else [(0, S)]:
+            for a, (lo, hi) in enumerate(HALVES):
                 nc.vector.tensor_tensor(
-                    h_rows[:, t, lo:hi],
-                    mem_sb[t][:].indirect(slot_sb[:, lo // 16 : hi // 16]),
-                    fade[lo // HALF] if hi - lo == HALF else fade_whole[:],
-                    ALU.mult,
+                    h_rows[a][:, t, :], mem_sb[t][:].indirect(slot_sb[:, lo // 16 : hi // 16]), fade[a], ALU.mult
                 )
 
         h_bf = []
         for lo, hi in PIECES:
             h_bf.append(keep.tile([P, hi - lo, PACK], BF16, name=f"h_bf{lo}", align_bytes=64))
-            interleave(nc.scalar.copy, h_bf[-1][:], h_rows[:, :, lo:hi])
+            interleave(nc.scalar.copy, h_bf[-1][:], h_rows[lo // HALF][:, :, lo % HALF : lo % HALF + hi - lo])
 
         def one_pass(group, w, codes, exps, first):
             nc.tensor.matmul_mx(
@@ -162,41 +167,32 @@ def tile_picked_ygrud_gate_p_kernel(tc, x_words, x_scales, mem, gap, rate, off, 
 
         acc = [psum.tile([N, hi - lo], F32, name=f"acc{lo}") for lo, hi in PIECES]
         rr_bf = reuse.tile([P, N, PACK], BF16, name="rr_bf", align_bytes=64, offset=RR_BF_AT)
-        x_codes = [
-            reuse.tile([P, HALF], U32, name="x_codes0", align_bytes=64, offset=X_CODES0_AT),
-            reuse.tile([P, P], U32, name="x_codes1", align_bytes=64, offset=X_CODES1_AT),
-            keep.tile([P, P], U32, name="x_codes2", tag="h_bf0", align_bytes=64),
-        ]
+        x_codes = reuse.tile([P, S], U32, name="x_codes", align_bytes=64, offset=X_CODES_AT)
 
-        def state_pass(i, first):
+        def quantize_state(i):
             lo, hi = PIECES[i]
             h_codes = keep.tile([P, hi - lo], U32, name=f"h_codes{lo}", align_bytes=64)
-            h_exps = reuse.tile([P, hi - lo], U8, name=f"h_exps{lo}", align_bytes=64, offset=RR_AT + lo)
+            h_exps = keep.tile([P, hi - lo], U8, name=f"h_exps{lo}", align_bytes=64)
             nc.vector.quantize_mx(
                 out=h_codes[:].bitcast(FP8X4), scales=h_exps[:], in_=h_bf[i][:].rearrange("p j t -> p (j t)")
             )
-            one_pass(acc[i][:], RR, h_codes[:], h_exps[:], first)
+            return h_codes, h_exps
 
-        def input_pass(i, first):
+        def finish(i, h_codes, h_exps):
             lo, hi = PIECES[i]
-            codes = x_codes[i][:]
-            nc.vector.tensor_copy(codes, words_sb[:].bitcast(U32).indirect(offs_sb[:, lo // 16 : hi // 16]))
-            one_pass(acc[i][:], W1, codes, x_exps[:, lo:hi], first)
-
-        def finish(i):
-            lo, hi = PIECES[i]
+            one_pass(acc[i][:], RR, h_codes[:], h_exps[:], False)
             gate = keep.tile([N, hi - lo], F32, name=f"gate{lo}")
             nc.scalar.activation(gate[:], acc[i][:], ACT.Sigmoid)
             queue = nc.scalar if hi == S else nc.sync
             queue.dma_start(out=out[:, lo:hi], in_=gate[:])
 
-        input_pass(0, True)
+        for lo, hi in HALVES:
+            nc.vector.tensor_copy(x_codes[:, lo:hi], words_sb[:].bitcast(U32).indirect(offs_sb[:, lo // 16 : hi // 16]))
+        for i, (lo, hi) in enumerate(PIECES):
+            one_pass(acc[i][:], W1, x_codes[:, lo:hi], x_exps[:, lo:hi], True)
         interleave(nc.vector.tensor_copy, rr_bf[:], rr_sb[:])
-        input_pass(1, True)
+        first_piece = quantize_state(0)
         quantize_weight(RR, rr_bf)
-        state_pass(0, False)
-        finish(0)
-        input_pass(2, True)
+        finish(0, *first_piece)
         for i in (1, 2):
-            state_pass(i, False)
-            finish(i)
+            finish(i, *quantize_state(i))

@@ -26,8 +26,10 @@ SCALE_ROWS_AT = 16
 
 X_CODES_AT = 0
 RR_BF_AT = 2048
-LAST_FADE_AT = 1536
-H_FIRST_AT = 3072
+MEM2_AT = 12288
+CLAMP_AT = [8192, 9216]
+PICKED_AT = {2: 10240, 3: 11264}
+H_FIRST_AT = 4096
 
 
 def interleave(copy, dst, src):
@@ -41,16 +43,17 @@ def tile_picked_ygrud_gate_p_kernel(tc, x_words, x_scales, mem, gap, rate, off, 
     nc = tc.nc
     with ExitStack() as ctx:
         keep = ctx.enter_context(tc.tile_pool(name="keep", bufs=1))
-        ring = ctx.enter_context(tc.tile_pool(name="ring", bufs=2))
         reuse = ctx.enter_context(tc.tile_pool(name="reuse", bufs=1))
         psum = ctx.enter_context(tc.psum_pool(name="psum", bufs=1))
 
         slot_sb = keep.tile([P, S // 16], U16, name="slot_sb")
         offs_sb = keep.tile([P, S // 16], U16, name="offs_sb")
         gap_col = keep.tile([P, 2, 8], F32, name="gap_col")
-        rate_sb = keep.tile([P, PACK], F32, name="rate_sb")
-        off_sb = keep.tile([P, PACK], F32, name="off_sb")
-        mem_sb = [keep.tile([P, U], F32, name=f"mem_sb{t}") for t in range(PACK)]
+        decay = keep.tile([P, 2, 8], F32, name="decay")
+        rate_sb, off_sb = decay[:, 0, 0:PACK], decay[:, 1, 0:PACK]
+        mem_sb = [keep.tile([P, U], F32, name=f"mem_sb{t}") for t in range(2)]
+        mem_sb.append(reuse.tile([P, U], F32, name="mem_sb2", align_bytes=64, offset=MEM2_AT))
+        mem_sb.append(reuse.tile([P, U], F32, name="mem_sb3", align_bytes=64, offset=X_CODES_AT))
         w1_sb = keep.tile([P, PACK, N], F32, name="w1_sb", tag="weight")
         rr_sb = keep.tile([P, PACK, N], F32, name="rr_sb", tag="weight")
         words_sb = keep.tile([P, T], I32, name="words_sb")
@@ -65,8 +68,8 @@ def tile_picked_ygrud_gate_p_kernel(tc, x_words, x_scales, mem, gap, rate, off, 
 
         mem_rows = mem.rearrange("(p t) u -> p t u", t=PACK)
         nc.sync.dma_start(out=gap_col[:, :, 0:2], in_=gap[0:1, :].rearrange("o (a p c) -> p (o a) c", a=2, c=2))
-        nc.scalar.dma_start(out=rate_sb[:], in_=rate.rearrange("(p t) o -> p (t o)", t=PACK))
-        nc.scalar.dma_start(out=off_sb[:], in_=off.rearrange("(p t) o -> p (t o)", t=PACK))
+        nc.scalar.dma_start(out=rate_sb, in_=rate.rearrange("(p t) o -> p (t o)", t=PACK))
+        nc.scalar.dma_start(out=off_sb, in_=off.rearrange("(p t) o -> p (t o)", t=PACK))
         nc.sync.dma_start(offs_sb[:], offs)
         nc.sync.dma_start(out=scales_sb[SCALE_ROWS_AT:32, :].bitcast(I32), in_=x_scales[0].bitcast(I32))
         nc.sync.dma_start(out=w1_sb[:], in_=w1.rearrange("(p t) n -> p t n", t=PACK))
@@ -112,46 +115,55 @@ def tile_picked_ygrud_gate_p_kernel(tc, x_words, x_scales, mem, gap, rate, off, 
         quantize_weight(W1, w1_bf)
         nc.sync.dma_start(out=rr_sb[:], in_=rr.rearrange("(p t) n -> p t n", t=PACK))
 
+        neg = {}
+        for t in (2, 3):
+            neg[t] = reuse.tile([P, 2], F32, name=f"neg{t}", align_bytes=64, offset=PICKED_AT[t])
+            nc.gpsimd.tensor_scalar(neg[t][:], decay[:, :, t], -1.0, 0.0, ALU.mult, ALU.add)
+
         h_rows = [
             reuse.tile([P, PACK, HALF], F32, name="h_rows0", align_bytes=64, offset=H_FIRST_AT),
             keep.tile([P, PACK, HALF], F32, name="h_rows1", align_bytes=64),
         ]
-        for t in range(PACK):
-            last_plane = t == PACK - 1
-            clamped = []
-            for a in range(2):
-                if last_plane:
-                    clamped.append(keep.tile([P, HALF], F32, name=f"last_clamped{a}"))
-                else:
-                    clamped.append(ring.tile([P, HALF], F32, name="clamped"))
+
+        def paired(view):
+            return view.rearrange("q (p c) -> q p c", c=2)
+
+        def half_list(a):
+            return slot_sb[:, a * HALF // 16 : (a + 1) * HALF // 16]
+
+        for pair in ([(0, 0), (0, 1)], [(1, 0), (1, 1)], [(2, 0), (3, 0)]):
+            clamped = [
+                reuse.tile([P, HALF], F32, name=f"clamped{t}{a}", align_bytes=64, offset=CLAMP_AT[i])
+                for i, (t, a) in enumerate(pair)
+            ]
+            fade = [keep.tile([P, HALF], F32, name=f"fade{t}{a}") for t, a in pair]
+            for i, (t, a) in enumerate(pair):
                 nc.scalar.activation(
-                    clamped[a][:].rearrange("q (p c) -> q p c", c=2),
-                    gap_halves[a],
-                    ACT.Relu,
-                    bias=off_sb[:, t : t + 1],
-                    scale=rate_sb[:, t : t + 1],
+                    paired(clamped[i][:]), gap_halves[a], ACT.Relu, bias=off_sb[:, t : t + 1], scale=rate_sb[:, t : t + 1]
                 )
-            if last_plane:
-                fade = [
-                    reuse.tile([P, HALF], F32, name="last_fade0", align_bytes=64, offset=LAST_FADE_AT)[:],
-                    keep.tile([P, HALF], F32, name="last_fade1")[:],
-                ]
-            else:
-                fade_whole = keep.tile([P, S], F32, name=f"fade{t}")
-                fade = [fade_whole[:, 0:HALF], fade_whole[:, HALF:S]]
-            for a in range(2):
-                nc.scalar.activation(fade[a], clamped[a][:], ACT.Exp, scale=-1.0)
-            if last_plane:
-                sigmoid_warm = keep.tile([P, 1], F32, name="sigmoid_warm")
-                nc.scalar.activation(sigmoid_warm[:], fade[1][:, HALF - 1 : HALF], ACT.Sigmoid)
-            for a, (lo, hi) in enumerate(HALVES):
-                nc.vector.tensor_tensor(
-                    h_rows[a][:, t, :], mem_sb[t][:].indirect(slot_sb[:, lo // 16 : hi // 16]), fade[a], ALU.mult
-                )
+            for i in range(2):
+                nc.scalar.activation(fade[i][:], clamped[i][:], ACT.Exp, scale=-1.0)
+            for i, (t, a) in enumerate(pair):
+                nc.vector.tensor_tensor(h_rows[a][:, t, :], mem_sb[t][:].indirect(half_list(a)), fade[i][:], ALU.mult)
+
+        growth, picked = {}, {}
+        for i, t in enumerate((2, 3)):
+            growth[t] = reuse.tile([P, HALF], F32, name=f"growth{t}", align_bytes=64, offset=CLAMP_AT[i])
+            nc.scalar.activation(
+                paired(growth[t][:]), gap_halves[1], ACT.Exp, bias=neg[t][:, 1:2], scale=neg[t][:, 0:1]
+            )
+        for t in (2, 3):
+            picked[t] = reuse.tile([P, HALF], F32, name=f"picked{t}", align_bytes=64, offset=PICKED_AT[t])
+            nc.scalar.activation(picked[t][:], mem_sb[t][:].indirect(half_list(1)), ACT.Copy)
+        for t in (2, 3):
+            nc.vector.scalar_tensor_tensor(h_rows[1][:, t, :], growth[t][:], 1.0, picked[t][:], ALU.min, ALU.mult)
 
         h_bf = []
         for lo, hi in PIECES:
-            h_bf.append(keep.tile([P, hi - lo, PACK], BF16, name=f"h_bf{lo}", align_bytes=64))
+            if lo == 0:
+                h_bf.append(reuse.tile([P, hi - lo, PACK], BF16, name="h_bf0", align_bytes=64, offset=MEM2_AT))
+            else:
+                h_bf.append(keep.tile([P, hi - lo, PACK], BF16, name=f"h_bf{lo}", align_bytes=64))
             interleave(nc.scalar.copy, h_bf[-1][:], h_rows[lo // HALF][:, :, lo % HALF : lo % HALF + hi - lo])
 
         def one_pass(group, w, codes, exps, first):
@@ -167,7 +179,18 @@ def tile_picked_ygrud_gate_p_kernel(tc, x_words, x_scales, mem, gap, rate, off, 
 
         acc = [psum.tile([N, hi - lo], F32, name=f"acc{lo}") for lo, hi in PIECES]
         rr_bf = reuse.tile([P, N, PACK], BF16, name="rr_bf", align_bytes=64, offset=RR_BF_AT)
-        x_codes = reuse.tile([P, S], U32, name="x_codes", align_bytes=64, offset=X_CODES_AT)
+        split = PIECES[-1][0]
+        x_codes = [
+            reuse.tile([P, split], U32, name="x_codes0", align_bytes=64, offset=X_CODES_AT),
+            reuse.tile([P, S - split], U32, name="x_codes1", align_bytes=64, offset=H_FIRST_AT + 1024),
+        ]
+
+        def observations(a):
+            lo, hi = ((0, split), (split, S))[a]
+            nc.vector.tensor_copy(x_codes[a][:], words_sb[:].bitcast(U32).indirect(offs_sb[:, lo // 16 : hi // 16]))
+            for i, (first, last) in enumerate(PIECES):
+                if lo <= first < hi:
+                    one_pass(acc[i][:], W1, x_codes[a][:, first - lo : last - lo], x_exps[:, first:last], True)
 
         def quantize_state(i):
             lo, hi = PIECES[i]
@@ -179,20 +202,23 @@ def tile_picked_ygrud_gate_p_kernel(tc, x_words, x_scales, mem, gap, rate, off, 
             return h_codes, h_exps
 
         def finish(i, h_codes, h_exps):
-            lo, hi = PIECES[i]
             one_pass(acc[i][:], RR, h_codes[:], h_exps[:], False)
-            gate = keep.tile([N, hi - lo], F32, name=f"gate{lo}")
-            nc.scalar.activation(gate[:], acc[i][:], ACT.Sigmoid)
-            queue = nc.scalar if hi == S else nc.sync
-            queue.dma_start(out=out[:, lo:hi], in_=gate[:])
 
-        for lo, hi in HALVES:
-            nc.vector.tensor_copy(x_codes[:, lo:hi], words_sb[:].bitcast(U32).indirect(offs_sb[:, lo // 16 : hi // 16]))
-        for i, (lo, hi) in enumerate(PIECES):
-            one_pass(acc[i][:], W1, x_codes[:, lo:hi], x_exps[:, lo:hi], True)
+        def store(i):
+            lo, hi = PIECES[i]
+            gate = keep.tile([N, hi - lo], F32, name=f"gate{lo}")
+            half_tanh = keep.tile([N, hi - lo], F32, name=f"half_tanh{lo}")
+            nc.scalar.activation(half_tanh[:], acc[i][:], ACT.Tanh, scale=0.5)
+            nc.vector.tensor_scalar(gate[:], half_tanh[:], 0.5, 0.5, ALU.mult, ALU.add)
+            nc.sync.dma_start(out=out[:, lo:hi], in_=gate[:])
+
+        observations(0)
         interleave(nc.vector.tensor_copy, rr_bf[:], rr_sb[:])
         first_piece = quantize_state(0)
         quantize_weight(RR, rr_bf)
         finish(0, *first_piece)
+        observations(1)
         for i in (1, 2):
             finish(i, *quantize_state(i))
+        for i in range(3):
+            store(i)

@@ -34,8 +34,8 @@ H_FIRST_AT = 4096
 
 def interleave(copy, dst, src):
     copy(
-        out=dst.rearrange("p (c i) t -> p c t i", i=2),
-        in_=src.rearrange("p t (c i) -> p c t i", i=2),
+        out=dst.rearrange("p (c i) t -> p c t i", i=4),
+        in_=src.rearrange("p t (c i) -> p c t i", i=4),
     )
 
 

@@ -54,8 +54,8 @@ def tile_picked_ygrud_gate_p_kernel(tc, x_words, x_scales, mem, gap, rate, off, 
         mem_sb = [keep.tile([P, U], F32, name=f"mem_sb{t}") for t in range(2)]
         mem_sb.append(reuse.tile([P, U], F32, name="mem_sb2", align_bytes=64, offset=MEM2_AT))
         mem_sb.append(reuse.tile([P, U], F32, name="mem_sb3", align_bytes=64, offset=X_CODES_AT))
-        w1_sb = keep.tile([P, PACK, N], F32, name="w1_sb", tag="weight")
-        rr_sb = keep.tile([P, PACK, N], F32, name="rr_sb", tag="weight")
+        w1_sb = keep.tile([P, PACK, N], F32, name="w1_sb")
+        rr_sb = keep.tile([P, PACK, N], F32, name="rr_sb")
         words_sb = keep.tile([P, T], I32, name="words_sb")
         scales_sb = keep.tile([P, T], U8, name="scales_sb")
         x_exps = keep.tile([P, S], U8, name="x_exps", align_bytes=64)
@@ -78,6 +78,7 @@ def tile_picked_ygrud_gate_p_kernel(tc, x_words, x_scales, mem, gap, rate, off, 
         for t in range(1, PACK):
             nc.sync.dma_start(out=mem_sb[t][:], in_=mem_rows[:, t, :])
         nc.sync.dma_start(out=words_sb[:], in_=x_words[0].rearrange("p c r -> p (c r)").bitcast(I32))
+        nc.sync.dma_start(out=rr_sb[:], in_=rr.rearrange("(p t) n -> p t n", t=PACK))
 
         nc.scalar.activation(exp_warm[:], exp_warm[:], ACT.Exp)
 
@@ -113,7 +114,6 @@ def tile_picked_ygrud_gate_p_kernel(tc, x_words, x_scales, mem, gap, rate, off, 
         w1_bf = keep.tile([P, N, PACK], BF16, name="w1_bf", align_bytes=64)
         interleave(nc.vector.tensor_copy, w1_bf[:], w1_sb[:])
         quantize_weight(W1, w1_bf)
-        nc.sync.dma_start(out=rr_sb[:], in_=rr.rearrange("(p t) n -> p t n", t=PACK))
 
         neg = {}
         for t in (2, 3):

from contextlib import ExitStack

import concourse.mybir as mybir
from concourse.masks import make_identity

K, T, S, H, N, U = 512, 1024, 512, 512, 128, 1024
FLOPS = 2 * (K + H) * N * S

F32 = mybir.dt.float32
BF16 = mybir.dt.bfloat16
I32 = mybir.dt.int32
U32 = mybir.dt.uint32
U16 = mybir.dt.uint16
U8 = mybir.dt.uint8
FP8X4 = mybir.dt.float8_e4m3fn_x4
ALU = mybir.AluOpType
ACT = mybir.ActivationFunctionType

P = 128
PACK = 4
HALF = S // 2
HALVES = [(0, HALF), (HALF, S)]
PIECES = [(0, 256), (256, 384), (384, 512)]
W1, RR = 0, 1
SCALE_ROWS_AT = 16

X_CODES_AT = 0
RR_BF_AT = 2048
MEM2_AT = 12288
CLAMP_AT = [8192, 9216]
PICKED_AT = {2: 10240, 3: 11264}
H_FIRST_AT = 4096


def interleave(copy, dst, src):
    copy(
        out=dst.rearrange("p (c i) t -> p c t i", i=4),
        in_=src.rearrange("p t (c i) -> p c t i", i=4),
    )


def tile_picked_ygrud_gate_p_kernel(tc, x_words, x_scales, mem, gap, rate, off, w1, rr, offs, slot, out):
    nc = tc.nc
    with ExitStack() as ctx:
        keep = ctx.enter_context(tc.tile_pool(name="keep", bufs=1))
        reuse = ctx.enter_context(tc.tile_pool(name="reuse", bufs=1))
        psum = ctx.enter_context(tc.psum_pool(name="psum", bufs=1))

        slot_sb = keep.tile([P, S // 16], U16, name="slot_sb")
        offs_sb = keep.tile([P, S // 16], U16, name="offs_sb")
        gap_col = keep.tile([P, 2, 8], F32, name="gap_col")
        decay = keep.tile([P, 2, 8], F32, name="decay")
        rate_sb, off_sb = decay[:, 0, 0:PACK], decay[:, 1, 0:PACK]
        mem_sb = [keep.tile([P, U], F32, name=f"mem_sb{t}") for t in range(2)]
        mem_sb.append(reuse.tile([P, U], F32, name="mem_sb2", align_bytes=64, offset=MEM2_AT))
        mem_sb.append(reuse.tile([P, U], F32, name="mem_sb3", align_bytes=64, offset=X_CODES_AT))
        w1_sb = keep.tile([P, PACK, N], F32, name="w1_sb")
        rr_sb = keep.tile([P, PACK, N], F32, name="rr_sb")
        words_sb = keep.tile([P, T], I32, name="words_sb")
        scales_sb = keep.tile([P, T], U8, name="scales_sb")
        x_exps = keep.tile([P, S], U8, name="x_exps", align_bytes=64)

        exp_warm = keep.tile([P, 1], F32, name="exp_warm")
        nc.vector.memset(exp_warm[:], 0.0)
        for first, last in [(0, SCALE_ROWS_AT), (32, 64), (64, P)]:
            nc.vector.memset(scales_sb[first:last, :].bitcast(I32), 0)
        nc.vector.memset(x_exps[:].bitcast(I32), 0)

        mem_rows = mem.rearrange("(p t) u -> p t u", t=PACK)
        nc.sync.dma_start(out=gap_col[:, :, 0:2], in_=gap[0:1, :].rearrange("o (a p c) -> p (o a) c", a=2, c=2))
        nc.scalar.dma_start(out=rate_sb, in_=rate.rearrange("(p t) o -> p (t o)", t=PACK))
        nc.scalar.dma_start(out=off_sb, in_=off.rearrange("(p t) o -> p (t o)", t=PACK))
        nc.sync.dma_start(offs_sb[:], offs)
        nc.sync.dma_start(out=scales_sb[SCALE_ROWS_AT:32, :].bitcast(I32), in_=x_scales[0].bitcast(I32))
        nc.sync.dma_start(out=w1_sb[:], in_=w1.rearrange("(p t) n -> p t n", t=PACK))
        nc.sync.dma_start(out=mem_sb[0][:], in_=mem_rows[:, 0, :])
        nc.sync.dma_start(slot_sb[:], slot)
        for t in range(1, PACK):
            nc.sync.dma_start(out=mem_sb[t][:], in_=mem_rows[:, t, :])
        nc.sync.dma_start(out=words_sb[:], in_=x_words[0].rearrange("p c r -> p (c r)").bitcast(I32))
        nc.sync.dma_start(out=rr_sb[:], in_=rr.rearrange("(p t) n -> p t n", t=PACK))

        nc.scalar.activation(exp_warm[:], exp_warm[:], ACT.Exp)

        ident = keep.tile([P, P], F32, name="ident")
        make_identity(nc, ident[:])
        gap_ps = [psum.tile([P, 2, P], F32, name=f"gap_ps{a}") for a in range(2)]
        for a in range(2):
            for c in range(2):
                nc.tensor.transpose(gap_ps[a][:, c, :], gap_col[:, a, c : c + 1].to_broadcast([P, P]), ident[:])

        picked_exps = keep.tile([P, S], U8, name="picked_exps")
        nc.vector.tensor_copy(picked_exps[:], scales_sb[:].indirect(offs_sb[:]))
        for q in range(4):
            row = SCALE_ROWS_AT + 4 * q
            nc.sync.dma_start(
                out=x_exps[32 * q : 32 * q + 4, :].bitcast(I32), in_=picked_exps[row : row + 4, :].bitcast(I32)
            )
        gap_halves = [gap_ps[a][:].rearrange("q c p -> q p c") for a in range(2)]

        w_codes = [keep.tile([P, N], U32, name=f"w_codes{w}", align_bytes=64) for w in (W1, RR)]
        w_exps = [
            keep.tile([P, N], U8, name="w1_exps", align_bytes=64),
            reuse.tile([P, N], U8, name="rr_exps", align_bytes=64, offset=H_FIRST_AT),
        ]

        def quantize_weight(w, w_bf):
            nc.vector.quantize_mx(
                out=w_codes[w][:].bitcast(FP8X4),
                scales=w_exps[w][:],
                in_=w_bf[:].rearrange("p n t -> p (n t)"),
            )

        w1_bf = keep.tile([P, N, PACK], BF16, name="w1_bf", align_bytes=64)
        interleave(nc.vector.tensor_copy, w1_bf[:], w1_sb[:])
        quantize_weight(W1, w1_bf)

        neg = {}
        for t in (2, 3):
            neg[t] = reuse.tile([P, 2], F32, name=f"neg{t}", align_bytes=64, offset=PICKED_AT[t])
            nc.gpsimd.tensor_scalar(neg[t][:], decay[:, :, t], -1.0, 0.0, ALU.mult, ALU.add)

        h_rows = [
            reuse.tile([P, PACK, HALF], F32, name="h_rows0", align_bytes=64, offset=H_FIRST_AT),
            keep.tile([P, PACK, HALF], F32, name="h_rows1", align_bytes=64),
        ]

        def paired(view):
            return view.rearrange("q (p c) -> q p c", c=2)

        def half_list(a):
            return slot_sb[:, a * HALF // 16 : (a + 1) * HALF // 16]

        for pair in ([(0, 0), (0, 1)], [(1, 0), (1, 1)], [(2, 0), (3, 0)]):
            clamped = [
                reuse.tile([P, HALF], F32, name=f"clamped{t}{a}", align_bytes=64, offset=CLAMP_AT[i])
                for i, (t, a) in enumerate(pair)
            ]
            fade = [keep.tile([P, HALF], F32, name=f"fade{t}{a}") for t, a in pair]
            for i, (t, a) in enumerate(pair):
                nc.scalar.activation(
                    paired(clamped[i][:]), gap_halves[a], ACT.Relu, bias=off_sb[:, t : t + 1], scale=rate_sb[:, t : t + 1]
                )
            for i in range(2):
                nc.scalar.activation(fade[i][:], clamped[i][:], ACT.Exp, scale=-1.0)
            for i, (t, a) in enumerate(pair):
                nc.vector.tensor_tensor(h_rows[a][:, t, :], mem_sb[t][:].indirect(half_list(a)), fade[i][:], ALU.mult)

        growth, picked = {}, {}
        for i, t in enumerate((2, 3)):
            growth[t] = reuse.tile([P, HALF], F32, name=f"growth{t}", align_bytes=64, offset=CLAMP_AT[i])
            nc.scalar.activation(
                paired(growth[t][:]), gap_halves[1], ACT.Exp, bias=neg[t][:, 1:2], scale=neg[t][:, 0:1]
            )
        for t in (2, 3):
            picked[t] = reuse.tile([P, HALF], F32, name=f"picked{t}", align_bytes=64, offset=PICKED_AT[t])
            nc.scalar.activation(picked[t][:], mem_sb[t][:].indirect(half_list(1)), ACT.Copy)
        for t in (2, 3):
            nc.vector.scalar_tensor_tensor(h_rows[1][:, t, :], growth[t][:], 1.0, picked[t][:], ALU.min, ALU.mult)

        h_bf = []
        for lo, hi in PIECES:
            if lo == 0:
                h_bf.append(reuse.tile([P, hi - lo, PACK], BF16, name="h_bf0", align_bytes=64, offset=MEM2_AT))
            else:
                h_bf.append(keep.tile([P, hi - lo, PACK], BF16, name=f"h_bf{lo}", align_bytes=64))
            interleave(nc.scalar.copy, h_bf[-1][:], h_rows[lo // HALF][:, :, lo % HALF : lo % HALF + hi - lo])

        def one_pass(group, w, codes, exps, first):
            nc.tensor.matmul_mx(
                out=group,
                lhsT=w_codes[w][:].bitcast(FP8X4),
                lhsT_scale=w_exps[w][:],
                rhs=codes.bitcast(FP8X4),
                rhs_scale=exps,
                start=first,
                stop=not first,
            )

        acc = [psum.tile([N, hi - lo], F32, name=f"acc{lo}") for lo, hi in PIECES]
        rr_bf = reuse.tile([P, N, PACK], BF16, name="rr_bf", align_bytes=64, offset=RR_BF_AT)
        split = PIECES[-1][0]
        x_codes = [
            reuse.tile([P, split], U32, name="x_codes0", align_bytes=64, offset=X_CODES_AT),
            reuse.tile([P, S - split], U32, name="x_codes1", align_bytes=64, offset=H_FIRST_AT + 1024),
        ]

        def observations(a):
            lo, hi = ((0, split), (split, S))[a]
            nc.vector.tensor_copy(x_codes[a][:], words_sb[:].bitcast(U32).indirect(offs_sb[:, lo // 16 : hi // 16]))
            for i, (first, last) in enumerate(PIECES):
                if lo <= first < hi:
                    one_pass(acc[i][:], W1, x_codes[a][:, first - lo : last - lo], x_exps[:, first:last], True)

        def quantize_state(i):
            lo, hi = PIECES[i]
            h_codes = keep.tile([P, hi - lo], U32, name=f"h_codes{lo}", align_bytes=64)
            h_exps = keep.tile([P, hi - lo], U8, name=f"h_exps{lo}", align_bytes=64)
            nc.vector.quantize_mx(
                out=h_codes[:].bitcast(FP8X4), scales=h_exps[:], in_=h_bf[i][:].rearrange("p j t -> p (j t)")
            )
            return h_codes, h_exps

        def finish(i, h_codes, h_exps):
            one_pass(acc[i][:], RR, h_codes[:], h_exps[:], False)

        def store(i):
            lo, hi = PIECES[i]
            gate = keep.tile([N, hi - lo], F32, name=f"gate{lo}")
            half_tanh = keep.tile([N, hi - lo], F32, name=f"half_tanh{lo}")
            nc.scalar.activation(half_tanh[:], acc[i][:], ACT.Tanh, scale=0.5)
            nc.vector.tensor_scalar(gate[:], half_tanh[:], 0.5, 0.5, ALU.mult, ALU.add)
            nc.sync.dma_start(out=out[:, lo:hi], in_=gate[:])

        observations(0)
        interleave(nc.vector.tensor_copy, rr_bf[:], rr_sb[:])
        first_piece = quantize_state(0)
        quantize_weight(RR, rr_bf)
        finish(0, *first_piece)
        observations(1)
        for i in (1, 2):
            finish(i, *quantize_state(i))
        for i in range(3):
            store(i)
